import numpy as np
import ml_dtypes


def mxq(x, axis, fmt="e4m3"):
    dtype, down = {"e4m3": (ml_dtypes.float8_e4m3fn, 7), "e5m2": (ml_dtypes.float8_e5m2, 14)}[fmt]
    v = np.moveaxis(np.asarray(x, np.float32).astype(ml_dtypes.bfloat16).astype(np.float64), axis, -1)
    blocks = v.reshape(v.shape[:-1] + (-1, 32))
    amax = np.abs(blocks).max(-1, keepdims=True)
    byte = np.maximum(np.where(amax > 0, np.frexp(amax)[1] - 1 + 127, 0) - down, 1)
    scale = np.exp2(byte - 127.0)
    codes = (blocks / scale).astype(np.float32).astype(dtype).astype(np.float64)
    return np.moveaxis((codes * scale).reshape(v.shape), -1, axis)


WIDE = False


def mx_kscale(k):
    if not WIDE:
        return np.ones(k)
    levels = np.array([24, -24, 12, -12, 0])
    if k % 512:
        return np.exp2(np.random.permutation(np.resize(levels, k // 32))).repeat(32)
    a = np.empty((k // 512, 16))
    for p in range(k // 512):
        a[p, :8] = np.random.permutation(np.resize(levels, 8))
        for g in range(8):
            far = levels[np.abs(levels - a[p, g]) >= 10]
            a[p, g + 8] = far[np.random.randint(len(far))]
    return np.exp2(a.ravel()).repeat(32)


def f64(x):
    return np.asarray(x).astype(np.float64)


def striped8(idx):
    return np.concatenate([v.reshape(-1, 16).T for v in idx]).astype(np.uint16)


def unstriped8(offs):
    return np.stack([offs[16 * g:16 * g + 16].T.reshape(-1) for g in range(8)]).astype(np.int64)


E2M1 = np.array([0.0, 0.5, 1.0, 1.5, 2.0, 3.0, 4.0, 6.0, -0.0, -0.5, -1.0, -1.5, -2.0, -3.0, -4.0, -6.0])


def pack_weight(w, fmt):
    k, n = w.shape
    w = f64(np.asarray(w, np.float32).astype(ml_dtypes.bfloat16)).reshape(k // 32, 32, n)
    amax = np.abs(w).max(1)
    if fmt == "e4m3":
        byte = np.frexp(amax)[1] - 1 + 127 - 7
    else:
        mant, ex = np.frexp(amax / 6.0)
        byte = np.where(mant > 0.5, ex, ex - 1) + 127
    byte = np.clip(np.where(amax > 0, byte, 1), 1, 254)
    scaled = (w * np.exp2(127.0 - byte)[:, None, :]).reshape(k, n).astype(np.float32)
    by_word = np.ascontiguousarray(scaled.reshape(k // 512, 128, 4, n).transpose(0, 1, 3, 2))
    if fmt == "e4m3":
        words = by_word.astype(ml_dtypes.float8_e4m3fn).view(np.uint8)
    else:
        c = by_word.astype(ml_dtypes.float4_e2m1fn).view(np.uint8) & 0xF
        words = (c[..., 0::2] | (c[..., 1::2] << 4)).reshape(k // 512, 128, 2 * n)
    return np.ascontiguousarray(words), np.ascontiguousarray(byte.astype(np.uint8).reshape(k // 512, 16, n))


def unpack_weight(words, scales, fmt):
    g, _, n = scales.shape
    words = np.ascontiguousarray(words).reshape(g, 128, n, -1)
    if fmt == "e4m3":
        vals = words.view(ml_dtypes.float8_e4m3fn).astype(np.float64)
    else:
        nib = np.empty((g, 128, n, 4), np.uint8)
        nib[..., 0::2] = words & 0xF
        nib[..., 1::2] = words >> 4
        vals = E2M1[nib]
    vals = vals * np.repeat(np.exp2(scales.astype(np.float64) - 127.0), 8, axis=1)[..., None]
    return vals.transpose(0, 1, 3, 2).reshape(g * 512, n)


def planes(y):
    n, m = y.shape
    v = y.astype(np.float32).astype(ml_dtypes.bfloat16).astype(np.float64).reshape(n // 32, 32, m)
    top = np.abs(v).max(1)
    byte = np.clip(np.where(top > 0, np.frexp(top)[1] - 1 + 127 - 7, 1), 1, 254)
    codes = (v * np.exp2(127.0 - byte)[:, None, :]).reshape(n, m).astype(np.float32).astype(ml_dtypes.float8_e4m3fn).view(np.uint8)
    words = codes.reshape(n // 512, 128, 4, m).transpose(0, 1, 3, 2)
    return np.ascontiguousarray(words), np.ascontiguousarray(byte.astype(np.uint8).reshape(n // 512, 16, m))


def sigm(f):
    return 1.0 / (1.0 + np.exp(-np.maximum(f, -700.0)))


K, R, N, T, J = 512, 1024, 512, 2048, 1024


def setup_inputs():
    n = np.random.standard_normal
    s = mx_kscale(K)[:, None]
    u = mx_kscale(R)[:, None]
    p_wg = pack_weight(n((K, R)) / np.sqrt(K) / s, "e4m3")
    p_wu = pack_weight(n((K, R)) / np.sqrt(K) / s * u.T, "e2m1")
    return {
        "xT": (n((K, T)) * s).astype(np.float32),
        "wgt": np.repeat(np.random.uniform(0.5, 2.0, (8, J)), 16, axis=0).astype(np.float32),
        "wg_words": p_wg[0],
        "wg_scales": p_wg[1],
        "wu_words": p_wu[0],
        "wu_scales": p_wu[1],
        "wd": (n((R, N)) / np.sqrt(R) / u).astype(np.float32),
        "offs": striped8(np.stack([np.random.permutation(T)[:J] for _ in range(8)])),
    }


def reference(xT, wgt, wg_words, wg_scales, wu_words, wu_scales, wd, offs):
    idx = unstriped8(offs)
    rows = np.arange(K)
    xg = f64(wgt)[rows // 4 % 128] * f64(xT)[rows[:, None], idx[rows % 512 // 64]]
    xT_ = mxq(xg, 0, "e4m3")
    wg_ = unpack_weight(wg_words, wg_scales, "e4m3")
    wu_ = unpack_weight(wu_words, wu_scales, "e2m1")
    ga = wg_.T @ xT_
    ub = wu_.T @ xT_
    h = sigm(ga) * ub
    h_ = mxq(h, 0, "e4m3")
    wd_ = mxq(f64(wd), 0, "e4m3")
    y = wd_.T @ h_
    return (y,) + planes(y)

@@ -1,0 +1,240 @@
+from contextlib import ExitStack
+
+import concourse.mybir as mybir
+
+K, R, N, T, J = 512, 1024, 512, 2048, 1024
+FLOPS = 2 * J * (2 * K * R + R * N)
+
+F32 = mybir.dt.float32
+BF16 = mybir.dt.bfloat16
+I32 = mybir.dt.int32
+U32 = mybir.dt.uint32
+U16 = mybir.dt.uint16
+U8 = mybir.dt.uint8
+FP8X4 = mybir.dt.float8_e4m3fn_x4
+FP4X4 = mybir.dt.float4_e2m1fn_x4
+MULT = mybir.AluOpType.mult
+SIGMOID = mybir.ActivationFunctionType.Sigmoid
+
+P = 128
+PACK = 4
+STEP = 128
+HALF = J // 2
+X_PARTS = [(0, 128), (128, 256), (256, 512), (512, 768), (768, 1024)]
+PASSES = R // (P * PACK)
+Y_MODE = "ssbbbbbv"
+
+
+def tile_list_sigm_noneP_kernel(
+    tc, xT, wgt, wg_words, wg_scales, wu_words, wu_scales, wd, offs, out_0, out_1, out_2
+):
+    nc = tc.nc
+    with ExitStack() as ctx:
+        keep = ctx.enter_context(tc.tile_pool(name="keep", bufs=1))
+        ring = ctx.enter_context(tc.tile_pool(name="ring", bufs=3))
+        psum = ctx.enter_context(tc.psum_pool(name="psum", bufs=3))
+
+        offsets = keep.tile([P, J // 16], U16, name="offsets")
+        nc.sync.dma_start(offsets[:], offs)
+        x_rows = xT.rearrange("(p i) t -> i p t", i=PACK)
+        x_plane = [keep.tile([P, T], F32, name="x_plane%d" % i) for i in range(PACK)]
+        nc.sync.dma_start(x_plane[0][:], x_rows[0])
+        weight = [keep.tile([P, HALF], F32, name="weight%d" % v) for v in range(2)]
+        for v in range(2):
+            nc.sync.dma_start(weight[v][:], wgt[:, HALF * v : HALF * (v + 1)])
+        nc.sync.dma_start(x_plane[1][:], x_rows[1])
+        nc.sync.dma_start(x_plane[2][:], x_rows[2])
+        wg_raw = keep.tile([P, R], I32, name="wg_raw")
+        nc.sync.dma_start(wg_raw[:], wg_words[0].rearrange("p r i -> p (r i)").bitcast(I32))
+        wu_raw = keep.tile([P, R // 2], I32, name="wu_raw")
+        nc.sync.dma_start(wu_raw[:], wu_words[0].bitcast(I32))
+        nc.sync.dma_start(x_plane[3][:], x_rows[3])
+        wd_raw = []
+        for b in range(PASSES):
+            raw = keep.tile([P, PACK, N], F32, name="wd_raw%d" % b)
+            rows = wd[512 * b : 512 * (b + 1), :].rearrange("(q t e) n -> t q e n", t=PACK, e=4)
+            for t in range(PACK):
+                nc.sync.dma_start(raw[:, t, :], rows[t])
+            wd_raw.append(raw)
+
+        warm = keep.tile([P, 1], F32, name="warm")
+        warm_out = keep.tile([P, 1], F32, name="warm_out")
+        nc.vector.memset(warm[:], 0.0)
+        nc.scalar.activation(warm_out[:], warm[:], SIGMOID)
+        scale_raw = keep.tile([P, R // 4], I32, name="scale_raw")
+        nc.vector.memset(scale_raw[:], 0)
+        for quad in range(4):
+            rows = slice(4 * quad, 4 * quad + 4)
+            nc.scalar.dma_start(scale_raw[32 * quad : 32 * quad + 4, :], wu_scales[0, rows, :].bitcast(I32))
+            nc.scalar.dma_start(scale_raw[32 * quad + 4 : 32 * quad + 8, :], wg_scales[0, rows, :].bitcast(I32))
+
+
+        picked = [keep.tile([P, 2, J], F32, name="picked%d" % u) for u in range(2)]
+        x_bf = [keep.tile([P, hi - lo, PACK], BF16, name="x_bf%d" % lo, align_bytes=64) for lo, hi in X_PARTS]
+        x_codes = keep.tile([P, J], U32, name="x_codes", align_bytes=64)
+        x_scales = keep.tile([P, J], U8, name="x_scales", align_bytes=64)
+
+        def gather(i, lo, hi):
+            window = x_plane[i][:].indirect(offsets[:, lo // 16 : hi // 16])
+            nc.vector.tensor_tensor(picked[i // 2][:, i % 2, lo:hi], window, weight[lo // HALF][:, lo % HALF : lo % HALF + hi - lo], MULT)
+
+        def pair_view(u, w):
+            src = picked[u][:, :, X_PARTS[w][0] : X_PARTS[w][1]].rearrange("p i j -> p j i")
+            return x_bf[w][:, :, 2 * u : 2 * u + 2], src
+
+        for i in range(2):
+            for v in range(2):
+                gather(i, HALF * v, HALF * (v + 1))
+        for w in range(len(X_PARTS)):
+            dst, src = pair_view(0, w)
+            nc.scalar.copy(dst, src)
+        for v in range(2):
+            gather(2, HALF * v, HALF * (v + 1))
+
+        def finish_x(w):
+            cols = slice(X_PARTS[w][0], X_PARTS[w][1])
+            gather(3, cols.start, cols.stop)
+            dst, src = pair_view(1, w)
+            nc.vector.tensor_copy(dst, src)
+            nc.vector.quantize_mx(
+                out=x_codes[:, cols].bitcast(FP8X4),
+                scales=x_scales[:, cols],
+                in_=x_bf[w][:].rearrange("p j i -> p (j i)"),
+            )
+
+        wg_codes = keep.tile([P, R], I32, name="wg_codes", align_bytes=64)
+        wu_codes = keep.tile([P, R // 2], I32, name="wu_codes", align_bytes=64)
+        w_scales = keep.tile([P, R // 4], I32, name="w_scales", align_bytes=64)
+
+        def deal(dst, src, words):
+            nc.vector.tensor_copy(
+                dst[:].rearrange("p (t q e) -> p t q e", t=PACK, e=words),
+                src[:].rearrange("p (q t e) -> p t q e", t=PACK, e=words),
+            )
+
+        wd_codes = keep.tile([P, PASSES, N], U32, name="wd_codes", align_bytes=64)
+        wd_scales = keep.tile([P, PASSES, N], U8, name="wd_scales", align_bytes=64)
+
+        def quantize_wd(b):
+            wd_bf = keep.tile([P, PACK, P, PACK], BF16, name="wd_bf%d" % b, align_bytes=64)
+            for half in range(2):
+                ms = slice(64 * half, 64 * (half + 1))
+                src = wd_raw[b][:].rearrange("p t (m i) -> p m t i", i=PACK)[:, ms, :, :]
+                dst = wd_bf[:].rearrange("p i m t -> p m t i")[:, ms, :, :]
+                nc.scalar.copy(dst, src)
+            nc.vector.quantize_mx(
+                out=wd_codes[:, b, :].bitcast(FP8X4),
+                scales=wd_scales[:, b, :],
+                in_=wd_bf[:].rearrange("p i m t -> p (i m t)"),
+            )
+
+        h_codes = [keep.tile([P, PASSES, STEP], U32, name="h_codes%d" % c, align_bytes=64) for c in range(J // STEP)]
+        h_scales = [keep.tile([P, PASSES, STEP], U8, name="h_scales%d" % c, align_bytes=64) for c in range(J // STEP)]
+
+        def hidden(c):
+            cols = slice(STEP * c, STEP * (c + 1))
+            h_bf = ring.tile([P, PASSES, STEP, PACK], BF16, name="h_bf", align_bytes=64)
+            for b in range(PASSES):
+                ga = psum.tile([P, PACK, STEP], F32, name="ga")
+                ub = psum.tile([P, PACK, STEP], F32, name="ub")
+                for t in range(PACK):
+                    first = t * (R // PACK) + b * P
+                    nc.tensor.matmul_mx(
+                        out=ga[:, t, :],
+                        lhsT=wg_codes[:, first : first + P].bitcast(FP8X4),
+                        lhsT_scale=w_scales[:].bitcast(U8)[4:P, first : first + P],
+                        rhs=x_codes[:, cols].bitcast(FP8X4),
+                        rhs_scale=x_scales[:, cols],
+                        start=True,
+                        stop=True,
+                    )
+                for t in range(PACK):
+                    first = t * (R // PACK) + b * P
+                    nc.tensor.matmul_mx(
+                        out=ub[:, t, :],
+                        lhsT=wu_codes[:].bitcast(U8)[:, 2 * first : 2 * (first + P)].bitcast(FP4X4),
+                        lhsT_scale=w_scales[:].bitcast(U8)[:, first : first + P],
+                        rhs=x_codes[:, cols].bitcast(FP8X4),
+                        rhs_scale=x_scales[:, cols],
+                        start=True,
+                        stop=True,
+                    )
+                gate = ring.tile([P, STEP, PACK], F32, name="gate")
+                nc.scalar.activation(gate[:], ga[:].rearrange("p t j -> p j t"), SIGMOID)
+                nc.vector.tensor_tensor(h_bf[:, b, :, :], ub[:].rearrange("p t j -> p j t"), gate[:], MULT)
+            nc.vector.quantize_mx(
+                out=h_codes[c][:].rearrange("p b j -> p (b j)").bitcast(FP8X4),
+                scales=h_scales[c][:].rearrange("p b j -> p (b j)"),
+                in_=h_bf[:].rearrange("p b j t -> p (b j t)"),
+            )
+
+        y_codes = keep.tile([P, J], U32, name="y_codes", align_bytes=64)
+        y_scales = keep.tile([P, J], U8, name="y_scales", align_bytes=64)
+        y_rows = out_0.rearrange("(p i) j -> p i j", i=PACK)
+        word_rows = out_1[0].rearrange("p j i -> p (j i)").bitcast(I32)
+
+        def output(c):
+            cols = slice(STEP * c, STEP * (c + 1))
+            acc = psum.tile([P, PACK, STEP], F32, name="acc", bufs=2)
+            for i in range(PACK):
+                for b in range(PASSES):
+                    nc.tensor.matmul_mx(
+                        out=acc[:, i, :],
+                        lhsT=wd_codes[:, b, P * i : P * (i + 1)].bitcast(FP8X4),
+                        lhsT_scale=wd_scales[:, b, P * i : P * (i + 1)],
+                        rhs=h_codes[c][:, b, :].bitcast(FP8X4),
+                        rhs_scale=h_scales[c][:, b, :],
+                        start=(b == 0),
+                        stop=(b == PASSES - 1),
+                    )
+            y = ring.tile([P, PACK, STEP], F32, name="y")
+            y_bf = ring.tile([P, STEP, PACK], BF16, name="y_bf", align_bytes=64)
+            if Y_MODE[c] == "b":
+                nc.scalar.copy(y[:], acc[:])
+                nc.vector.tensor_copy(
+                    y_bf[:].rearrange("p (s u) i -> p s i u", u=4),
+                    y[:].rearrange("p i (s u) -> p s i u", u=4),
+                )
+            elif Y_MODE[c] == "v":
+                nc.vector.tensor_copy(y_bf[:], acc[:].rearrange("p i j -> p j i"))
+                nc.scalar.copy(y[:], acc[:])
+            else:
+                nc.scalar.copy(y_bf[:], acc[:].rearrange("p i j -> p j i"))
+                nc.scalar.copy(y[:], acc[:])
+            nc.sync.dma_start(y_rows[:, :, cols], y[:])
+            nc.vector.quantize_mx(
+                out=y_codes[:, cols].bitcast(FP8X4),
+                scales=y_scales[:, cols],
+                in_=y_bf[:].rearrange("p j i -> p (j i)"),
+            )
+            if c % 2 == 1:
+                both = slice(STEP * (c - 1), STEP * (c + 1))
+                nc.sync.dma_start(word_rows[:, both], y_codes[:, both].bitcast(I32))
+
+        deal(w_scales, scale_raw, 1)
+        deal(wg_codes, wg_raw, 4)
+        deal(wu_codes, wu_raw, 2)
+        finish_x(0)
+        finish_x(1)
+        hidden(0)
+        finish_x(2)
+        hidden(1)
+        quantize_wd(0)
+        hidden(2)
+        finish_x(3)
+        quantize_wd(1)
+        hidden(3)
+        finish_x(4)
+        output(0)
+        for c in range(4, J // STEP):
+            hidden(c)
+            output(c - 3)
+        for c in range(J // STEP - 3, J // STEP):
+            output(c)
+
+        for quad in range(4):
+            queue = nc.scalar if quad % 2 else nc.sync
+            queue.dma_start(
+                out_2[0, 4 * quad : 4 * quad + 4, :].bitcast(I32),
+                y_scales[32 * quad : 32 * quad + 4, :].bitcast(I32),
+            )

@@ -20,9 +20,14 @@ P = 128
 PACK = 4
 STEP = 128
 HALF = J // 2
-X_PARTS = [(0, 128), (128, 256), (256, 512), (512, 768), (768, 1024)]
+HEAD = 256
+X_PARTS = [(0, 256), (256, 512), (512, 768), (768, 1024)]
+H_PARTS = [(0, 2), (2, 4), (4, 6), (6, 7), (7, 8)]
+Y_PARTS = [(0, 2), (2, 4), (4, 6), (6, 7), (7, 8)]
 PASSES = R // (P * PACK)
-Y_MODE = "ssbbbbbv"
+X_MODE = "ssss"
+W_MODE = "vvvv"
+Y_MODE = "sssbbbbb"
 
 
 def tile_list_sigm_noneP_kernel(
@@ -31,21 +36,32 @@ def tile_list_sigm_noneP_kernel(
     nc = tc.nc
     with ExitStack() as ctx:
         keep = ctx.enter_context(tc.tile_pool(name="keep", bufs=1))
-        ring = ctx.enter_context(tc.tile_pool(name="ring", bufs=3))
+        ring = ctx.enter_context(tc.tile_pool(name="ring", bufs=8))
         psum = ctx.enter_context(tc.psum_pool(name="psum", bufs=3))
 
         offsets = keep.tile([P, J // 16], U16, name="offsets")
-        nc.sync.dma_start(offsets[:], offs)
+        scale_raw = keep.tile([P, R // 4], I32, name="scale_raw")
+        nc.vector.memset(scale_raw[:], 0)
+
+        def load_scales(source, first_row, quads):
+            for quad in quads:
+                rows = slice(32 * quad + first_row, 32 * quad + first_row + 4)
+                nc.sync.dma_start(scale_raw[rows, :], source[0, 4 * quad : 4 * quad + 4, :].bitcast(I32))
+
         x_rows = xT.rearrange("(p i) t -> i p t", i=PACK)
         x_plane = [keep.tile([P, T], F32, name="x_plane%d" % i) for i in range(PACK)]
         nc.sync.dma_start(x_plane[0][:], x_rows[0])
-        weight = [keep.tile([P, HALF], F32, name="weight%d" % v) for v in range(2)]
-        for v in range(2):
-            nc.sync.dma_start(weight[v][:], wgt[:, HALF * v : HALF * (v + 1)])
+        nc.sync.dma_start(offsets[:], offs)
+        weight = keep.tile([P, J], F32, name="weight")
+        nc.sync.dma_start(weight[:, 0:HEAD], wgt[:, 0:HEAD])
+        nc.sync.dma_start(weight[:, HEAD:J], wgt[:, HEAD:J])
         nc.sync.dma_start(x_plane[1][:], x_rows[1])
+        load_scales(wu_scales, 0, range(4))
+        load_scales(wg_scales, 4, range(2))
         nc.sync.dma_start(x_plane[2][:], x_rows[2])
         wg_raw = keep.tile([P, R], I32, name="wg_raw")
         nc.sync.dma_start(wg_raw[:], wg_words[0].rearrange("p r i -> p (r i)").bitcast(I32))
+        load_scales(wg_scales, 4, range(2, 4))
         wu_raw = keep.tile([P, R // 2], I32, name="wu_raw")
         nc.sync.dma_start(wu_raw[:], wu_words[0].bitcast(I32))
         nc.sync.dma_start(x_plane[3][:], x_rows[3])
@@ -61,54 +77,41 @@ def tile_list_sigm_noneP_kernel(
         warm_out = keep.tile([P, 1], F32, name="warm_out")
         nc.vector.memset(warm[:], 0.0)
         nc.scalar.activation(warm_out[:], warm[:], SIGMOID)
-        scale_raw = keep.tile([P, R // 4], I32, name="scale_raw")
-        nc.vector.memset(scale_raw[:], 0)
-        for quad in range(4):
-            rows = slice(4 * quad, 4 * quad + 4)
-            nc.scalar.dma_start(scale_raw[32 * quad : 32 * quad + 4, :], wu_scales[0, rows, :].bitcast(I32))
-            nc.scalar.dma_start(scale_raw[32 * quad + 4 : 32 * quad + 8, :], wg_scales[0, rows, :].bitcast(I32))
-
-
-        picked = [keep.tile([P, 2, J], F32, name="picked%d" % u) for u in range(2)]
-        x_bf = [keep.tile([P, hi - lo, PACK], BF16, name="x_bf%d" % lo, align_bytes=64) for lo, hi in X_PARTS]
+        picked = [keep.tile([P, PACK, HALF], F32, name="picked%d" % v, align_bytes=64) for v in range(2)]
+        x_bf = []
+        for w, (lo, hi) in enumerate(X_PARTS):
+            x_bf.append(keep.tile([P, PACK * (hi - lo)], BF16, name="x_bf%d" % lo, align_bytes=64)[:])
         x_codes = keep.tile([P, J], U32, name="x_codes", align_bytes=64)
         x_scales = keep.tile([P, J], U8, name="x_scales", align_bytes=64)
 
         def gather(i, lo, hi):
+            inner = slice(lo % HALF, lo % HALF + hi - lo)
             window = x_plane[i][:].indirect(offsets[:, lo // 16 : hi // 16])
-            nc.vector.tensor_tensor(picked[i // 2][:, i % 2, lo:hi], window, weight[lo // HALF][:, lo % HALF : lo % HALF + hi - lo], MULT)
+            nc.vector.tensor_tensor(picked[lo // HALF][:, i, inner], window, weight[:, lo:hi], MULT)
 
-        def pair_view(u, w):
-            src = picked[u][:, :, X_PARTS[w][0] : X_PARTS[w][1]].rearrange("p i j -> p j i")
-            return x_bf[w][:, :, 2 * u : 2 * u + 2], src
-
-        for i in range(2):
-            for v in range(2):
-                gather(i, HALF * v, HALF * (v + 1))
-        for w in range(len(X_PARTS)):
-            dst, src = pair_view(0, w)
-            nc.scalar.copy(dst, src)
-        for v in range(2):
-            gather(2, HALF * v, HALF * (v + 1))
+        gather(0, 0, HEAD)
+        gather(0, HEAD, HALF)
+        gather(0, HALF, J)
+        for i in range(1, PACK - 1):
+            for lo in range(0, J, HALF):
+                gather(i, lo, lo + HALF)
 
         def finish_x(w):
-            cols = slice(X_PARTS[w][0], X_PARTS[w][1])
-            gather(3, cols.start, cols.stop)
-            dst, src = pair_view(1, w)
-            nc.vector.tensor_copy(dst, src)
-            nc.vector.quantize_mx(
-                out=x_codes[:, cols].bitcast(FP8X4),
-                scales=x_scales[:, cols],
-                in_=x_bf[w][:].rearrange("p j i -> p (j i)"),
-            )
+            lo, hi = X_PARTS[w]
+            gather(PACK - 1, lo, hi)
+            src = picked[lo // HALF][:, :, lo % HALF : lo % HALF + hi - lo].rearrange("p i (s u) -> p s i u", u=4)
+            dst = x_bf[w].rearrange("p (s u i) -> p s i u", u=4, i=PACK)
+            if X_MODE[w] == "s":
+                nc.scalar.copy(dst, src)
+            else:
+                nc.vector.tensor_copy(dst, src)
+            nc.vector.quantize_mx(out=x_codes[:, lo:hi].bitcast(FP8X4), scales=x_scales[:, lo:hi], in_=x_bf[w])
 
-        wg_codes = keep.tile([P, R], I32, name="wg_codes", align_bytes=64)
-        wu_codes = keep.tile([P, R // 2], I32, name="wu_codes", align_bytes=64)
         w_scales = keep.tile([P, R // 4], I32, name="w_scales", align_bytes=64)
 
         def deal(dst, src, words):
             nc.vector.tensor_copy(
-                dst[:].rearrange("p (t q e) -> p t q e", t=PACK, e=words),
+                dst.rearrange("p (t q e) -> p t q e", t=PACK, e=words),
                 src[:].rearrange("p (q t e) -> p t q e", t=PACK, e=words),
             )
 
@@ -121,19 +124,28 @@ def tile_list_sigm_noneP_kernel(
                 ms = slice(64 * half, 64 * (half + 1))
                 src = wd_raw[b][:].rearrange("p t (m i) -> p m t i", i=PACK)[:, ms, :, :]
                 dst = wd_bf[:].rearrange("p i m t -> p m t i")[:, ms, :, :]
-                nc.scalar.copy(dst, src)
+                if W_MODE[2 * b + half] == "s":
+                    nc.scalar.copy(dst, src)
+                else:
+                    nc.vector.tensor_copy(dst, src)
             nc.vector.quantize_mx(
                 out=wd_codes[:, b, :].bitcast(FP8X4),
                 scales=wd_scales[:, b, :],
                 in_=wd_bf[:].rearrange("p i m t -> p (i m t)"),
             )
 
-        h_codes = [keep.tile([P, PASSES, STEP], U32, name="h_codes%d" % c, align_bytes=64) for c in range(J // STEP)]
-        h_scales = [keep.tile([P, PASSES, STEP], U8, name="h_scales%d" % c, align_bytes=64) for c in range(J // STEP)]
+        h_codes, h_scales, h_stage = {}, {}, {}
+        for lo, hi in H_PARTS:
+            codes = keep.tile([P, hi - lo, PASSES, STEP], U32, name="h_codes%d" % lo, align_bytes=64)
+            scales = keep.tile([P, hi - lo, PASSES, STEP], U8, name="h_scales%d" % lo, align_bytes=64)
+            stage = keep.tile([P, hi - lo, PASSES, STEP, PACK], BF16, name="h_bf%d" % lo, align_bytes=64)
+            for c in range(lo, hi):
+                h_codes[c], h_scales[c], h_stage[c] = codes[:, c - lo, :, :], scales[:, c - lo, :, :], stage[:, c - lo, :, :, :]
+            h_stage[lo, hi] = (codes, scales, stage)
 
         def hidden(c):
             cols = slice(STEP * c, STEP * (c + 1))
-            h_bf = ring.tile([P, PASSES, STEP, PACK], BF16, name="h_bf", align_bytes=64)
+            h_bf = h_stage[c]
             for b in range(PASSES):
                 ga = psum.tile([P, PACK, STEP], F32, name="ga")
                 ub = psum.tile([P, PACK, STEP], F32, name="ub")
@@ -152,7 +164,7 @@ def tile_list_sigm_noneP_kernel(
                     first = t * (R // PACK) + b * P
                     nc.tensor.matmul_mx(
                         out=ub[:, t, :],
-                        lhsT=wu_codes[:].bitcast(U8)[:, 2 * first : 2 * (first + P)].bitcast(FP4X4),
+                        lhsT=wu_codes.bitcast(U8)[:, 2 * first : 2 * (first + P)].bitcast(FP4X4),
                         lhsT_scale=w_scales[:].bitcast(U8)[:, first : first + P],
                         rhs=x_codes[:, cols].bitcast(FP8X4),
                         rhs_scale=x_scales[:, cols],
@@ -162,19 +174,28 @@ def tile_list_sigm_noneP_kernel(
                 gate = ring.tile([P, STEP, PACK], F32, name="gate")
                 nc.scalar.activation(gate[:], ga[:].rearrange("p t j -> p j t"), SIGMOID)
                 nc.vector.tensor_tensor(h_bf[:, b, :, :], ub[:].rearrange("p t j -> p j t"), gate[:], MULT)
-            nc.vector.quantize_mx(
-                out=h_codes[c][:].rearrange("p b j -> p (b j)").bitcast(FP8X4),
-                scales=h_scales[c][:].rearrange("p b j -> p (b j)"),
-                in_=h_bf[:].rearrange("p b j t -> p (b j t)"),
-            )
+            for lo, hi in H_PARTS:
+                if hi == c + 1:
+                    codes, scales, stage = h_stage[lo, hi]
+                    nc.vector.quantize_mx(
+                        out=codes[:].rearrange("p c b j -> p (c b j)").bitcast(FP8X4),
+                        scales=scales[:].rearrange("p c b j -> p (c b j)"),
+                        in_=stage[:].rearrange("p c b j t -> p (c b j t)"),
+                    )
 
         y_codes = keep.tile([P, J], U32, name="y_codes", align_bytes=64)
         y_scales = keep.tile([P, J], U8, name="y_scales", align_bytes=64)
         y_rows = out_0.rearrange("(p i) j -> p i j", i=PACK)
         word_rows = out_1[0].rearrange("p j i -> p (j i)").bitcast(I32)
 
+        y_stage = {}
+        for lo, hi in Y_PARTS:
+            whole = keep.tile([P, PACK, STEP * (hi - lo)], F32, name="y%d" % lo)
+            whole_bf = keep.tile([P, STEP * (hi - lo), PACK], BF16, name="y_bf%d" % lo, align_bytes=64)
+            for c in range(lo, hi):
+                y_stage[c] = (lo, hi, whole, whole_bf)
+
         def output(c):
-            cols = slice(STEP * c, STEP * (c + 1))
             acc = psum.tile([P, PACK, STEP], F32, name="acc", bufs=2)
             for i in range(PACK):
                 for b in range(PASSES):
@@ -187,49 +208,51 @@ def tile_list_sigm_noneP_kernel(
                         start=(b == 0),
                         stop=(b == PASSES - 1),
                     )
-            y = ring.tile([P, PACK, STEP], F32, name="y")
-            y_bf = ring.tile([P, STEP, PACK], BF16, name="y_bf", align_bytes=64)
+            lo, hi, whole, whole_bf = y_stage[c]
+            inner = slice(STEP * (c - lo), STEP * (c - lo + 1))
+            y = whole[:, :, inner]
+            y_bf = whole_bf[:, inner, :]
             if Y_MODE[c] == "b":
-                nc.scalar.copy(y[:], acc[:])
+                nc.scalar.copy(y, acc[:])
                 nc.vector.tensor_copy(
-                    y_bf[:].rearrange("p (s u) i -> p s i u", u=4),
-                    y[:].rearrange("p i (s u) -> p s i u", u=4),
+                    y_bf.rearrange("p (s u) i -> p s i u", u=4),
+                    y.rearrange("p i (s u) -> p s i u", u=4),
                 )
             elif Y_MODE[c] == "v":
-                nc.vector.tensor_copy(y_bf[:], acc[:].rearrange("p i j -> p j i"))
-                nc.scalar.copy(y[:], acc[:])
+                nc.vector.tensor_copy(y_bf, acc[:].rearrange("p i j -> p j i"))
+                nc.scalar.copy(y, acc[:])
             else:
-                nc.scalar.copy(y_bf[:], acc[:].rearrange("p i j -> p j i"))
-                nc.scalar.copy(y[:], acc[:])
-            nc.sync.dma_start(y_rows[:, :, cols], y[:])
-            nc.vector.quantize_mx(
-                out=y_codes[:, cols].bitcast(FP8X4),
-                scales=y_scales[:, cols],
-                in_=y_bf[:].rearrange("p j i -> p (j i)"),
-            )
-            if c % 2 == 1:
-                both = slice(STEP * (c - 1), STEP * (c + 1))
-                nc.sync.dma_start(word_rows[:, both], y_codes[:, both].bitcast(I32))
+                nc.scalar.copy(y_bf, acc[:].rearrange("p i j -> p j i"))
+                nc.scalar.copy(y, acc[:])
+            if c + 1 == hi:
+                cols = slice(STEP * lo, STEP * hi)
+                nc.sync.dma_start(y_rows[:, :, cols], whole[:])
+                nc.vector.quantize_mx(
+                    out=y_codes[:, cols].bitcast(FP8X4),
+                    scales=y_scales[:, cols],
+                    in_=whole_bf[:].rearrange("p j i -> p (j i)"),
+                )
+                nc.sync.dma_start(word_rows[:, cols], y_codes[:, cols].bitcast(I32))
 
-        deal(w_scales, scale_raw, 1)
+        deal(w_scales[:], scale_raw, 1)
+        finish_x(0)
+        wg_codes = keep.tile([P, R], I32, name="wg_codes", align_bytes=64)[:]
+        wu_codes = keep.tile([P, R // 2], I32, name="wu_codes", align_bytes=64)[:]
         deal(wg_codes, wg_raw, 4)
         deal(wu_codes, wu_raw, 2)
-        finish_x(0)
         finish_x(1)
         hidden(0)
-        finish_x(2)
         hidden(1)
-        quantize_wd(0)
+        finish_x(2)
         hidden(2)
-        finish_x(3)
+        quantize_wd(0)
         quantize_wd(1)
+        finish_x(3)
         hidden(3)
-        finish_x(4)
-        output(0)
         for c in range(4, J // STEP):
             hidden(c)
-            output(c - 3)
-        for c in range(J // STEP - 3, J // STEP):
+            output(c - 4)
+        for c in range(J // STEP - 4, J // STEP):
             output(c)
 
         for quad in range(4):

@@ -14,20 +14,21 @@ U8 = mybir.dt.uint8
 FP8X4 = mybir.dt.float8_e4m3fn_x4
 FP4X4 = mybir.dt.float4_e2m1fn_x4
 MULT = mybir.AluOpType.mult
+ADD = mybir.AluOpType.add
 SIGMOID = mybir.ActivationFunctionType.Sigmoid
 
 P = 128
 PACK = 4
 STEP = 128
-HALF = J // 2
+BANK = 512
 HEAD = 256
-X_PARTS = [(0, 256), (256, 512), (512, 768), (768, 1024)]
-H_PARTS = [(0, 2), (2, 4), (4, 6), (6, 7), (7, 8)]
-Y_PARTS = [(0, 2), (2, 4), (4, 6), (6, 7), (7, 8)]
 PASSES = R // (P * PACK)
+X_PARTS = [(0, 256), (256, 512), (512, 768), (768, 1024)]
+GROUPS = [(0, 2), (2, 4), (4, 5), (5, 6), (6, 7), (7, 8)]
+X_REUSE = {0: 3}
 X_MODE = "ssss"
 W_MODE = "vvvv"
-Y_MODE = "sssbbbbb"
+Y_MODE = "ssssvvvv"
 
 
 def tile_list_sigm_noneP_kernel(
@@ -37,83 +38,103 @@ def tile_list_sigm_noneP_kernel(
     with ExitStack() as ctx:
         keep = ctx.enter_context(tc.tile_pool(name="keep", bufs=1))
         ring = ctx.enter_context(tc.tile_pool(name="ring", bufs=8))
-        psum = ctx.enter_context(tc.psum_pool(name="psum", bufs=3))
+        psum = ctx.enter_context(tc.psum_pool(name="psum", bufs=1))
 
         offsets = keep.tile([P, J // 16], U16, name="offsets")
         scale_raw = keep.tile([P, R // 4], I32, name="scale_raw")
         nc.vector.memset(scale_raw[:], 0)
 
-        def load_scales(source, first_row, quads):
-            for quad in quads:
+        def load_scales(queue, source, first_row):
+            for quad in range(4):
                 rows = slice(32 * quad + first_row, 32 * quad + first_row + 4)
-                nc.sync.dma_start(scale_raw[rows, :], source[0, 4 * quad : 4 * quad + 4, :].bitcast(I32))
+                queue.dma_start(scale_raw[rows, :], source[0, 4 * quad : 4 * quad + 4, :].bitcast(I32))
 
         x_rows = xT.rearrange("(p i) t -> i p t", i=PACK)
         x_plane = [keep.tile([P, T], F32, name="x_plane%d" % i) for i in range(PACK)]
-        nc.sync.dma_start(x_plane[0][:], x_rows[0])
-        nc.sync.dma_start(offsets[:], offs)
         weight = keep.tile([P, J], F32, name="weight")
-        nc.sync.dma_start(weight[:, 0:HEAD], wgt[:, 0:HEAD])
-        nc.sync.dma_start(weight[:, HEAD:J], wgt[:, HEAD:J])
-        nc.sync.dma_start(x_plane[1][:], x_rows[1])
-        load_scales(wu_scales, 0, range(4))
-        load_scales(wg_scales, 4, range(2))
-        nc.sync.dma_start(x_plane[2][:], x_rows[2])
-        wg_raw = keep.tile([P, R], I32, name="wg_raw")
-        nc.sync.dma_start(wg_raw[:], wg_words[0].rearrange("p r i -> p (r i)").bitcast(I32))
-        load_scales(wg_scales, 4, range(2, 4))
-        wu_raw = keep.tile([P, R // 2], I32, name="wu_raw")
-        nc.sync.dma_start(wu_raw[:], wu_words[0].bitcast(I32))
-        nc.sync.dma_start(x_plane[3][:], x_rows[3])
-        wd_raw = []
-        for b in range(PASSES):
-            raw = keep.tile([P, PACK, N], F32, name="wd_raw%d" % b)
+        wg_raw = [keep.tile([P, BANK], I32, name="wg_raw%d" % b) for b in range(PASSES)]
+        wu_raw = [keep.tile([P, BANK // 2], I32, name="wu_raw%d" % b) for b in range(PASSES)]
+        wd_raw = [keep.tile([P, PACK, N], F32, name="wd_raw%d" % b) for b in range(PASSES)]
+        wg_hbm = wg_words[0].rearrange("p r i -> p (r i)").bitcast(I32)
+        wu_hbm = wu_words[0].bitcast(I32)
+
+        def load_x(i):
+            nc.sync.dma_start(x_plane[i][:], x_rows[i])
+
+        def load_packed(b):
+            nc.sync.dma_start(wg_raw[b][:], wg_hbm[:, 512 * b : 512 * (b + 1)])
+            nc.sync.dma_start(wu_raw[b][:], wu_hbm[:, 256 * b : 256 * (b + 1)])
+
+        def load_wd(b):
             rows = wd[512 * b : 512 * (b + 1), :].rearrange("(q t e) n -> t q e n", t=PACK, e=4)
             for t in range(PACK):
-                nc.sync.dma_start(raw[:, t, :], rows[t])
-            wd_raw.append(raw)
+                nc.sync.dma_start(wd_raw[b][:, t, :], rows[t])
+
+        load_x(0)
+        nc.sync.dma_start(offsets[:], offs)
+        nc.sync.dma_start(weight[:, 0:HEAD], wgt[:, 0:HEAD])
+        nc.sync.dma_start(weight[:, HEAD:J], wgt[:, HEAD:J])
+        load_x(1)
+        load_scales(nc.sync, wu_scales, 0)
+        load_x(2)
+        load_scales(nc.sync, wg_scales, 4)
+        load_x(3)
+        load_packed(0)
+        load_packed(1)
+        load_wd(0)
+        load_wd(1)
 
         warm = keep.tile([P, 1], F32, name="warm")
         warm_out = keep.tile([P, 1], F32, name="warm_out")
         nc.vector.memset(warm[:], 0.0)
         nc.scalar.activation(warm_out[:], warm[:], SIGMOID)
-        picked = [keep.tile([P, PACK, HALF], F32, name="picked%d" % v, align_bytes=64) for v in range(2)]
-        x_bf = []
-        for w, (lo, hi) in enumerate(X_PARTS):
-            x_bf.append(keep.tile([P, PACK * (hi - lo)], BF16, name="x_bf%d" % lo, align_bytes=64)[:])
+
+        def cast(mode, dst, src):
+            if mode == "s":
+                nc.scalar.copy(dst, src)
+            elif mode == "g":
+                nc.gpsimd.tensor_scalar(dst, src, 1.0, 0.0, MULT, ADD)
+            else:
+                nc.vector.tensor_copy(dst, src)
+
+        picked = [keep.tile([P, PACK + 1, hi - lo], F32, name="picked%d" % lo, align_bytes=64) for lo, hi in X_PARTS]
         x_codes = keep.tile([P, J], U32, name="x_codes", align_bytes=64)
         x_scales = keep.tile([P, J], U8, name="x_scales", align_bytes=64)
 
-        def gather(i, lo, hi):
-            inner = slice(lo % HALF, lo % HALF + hi - lo)
+        def gather(i, w):
+            lo, hi = X_PARTS[w]
             window = x_plane[i][:].indirect(offsets[:, lo // 16 : hi // 16])
-            nc.vector.tensor_tensor(picked[lo // HALF][:, i, inner], window, weight[:, lo:hi], MULT)
+            nc.vector.tensor_tensor(picked[w][:, i, :], window, weight[:, lo:hi], MULT)
 
-        gather(0, 0, HEAD)
-        gather(0, HEAD, HALF)
-        gather(0, HALF, J)
-        for i in range(1, PACK - 1):
-            for lo in range(0, J, HALF):
-                gather(i, lo, lo + HALF)
+        for i in range(PACK - 1):
+            for w in range(len(X_PARTS)):
+                gather(i, w)
 
         def finish_x(w):
             lo, hi = X_PARTS[w]
-            gather(PACK - 1, lo, hi)
-            src = picked[lo // HALF][:, :, lo % HALF : lo % HALF + hi - lo].rearrange("p i (s u) -> p s i u", u=4)
-            dst = x_bf[w].rearrange("p (s u i) -> p s i u", u=4, i=PACK)
-            if X_MODE[w] == "s":
-                nc.scalar.copy(dst, src)
+            gather(PACK - 1, w)
+            if w in X_REUSE:
+                x_bf = picked[X_REUSE[w]][:, PACK - 1 :, :].rearrange("p a j -> p (a j)")[:, 0 : 2 * (hi - lo)].bitcast(BF16)
             else:
-                nc.vector.tensor_copy(dst, src)
-            nc.vector.quantize_mx(out=x_codes[:, lo:hi].bitcast(FP8X4), scales=x_scales[:, lo:hi], in_=x_bf[w])
+                x_bf = keep.tile([P, PACK * (hi - lo)], BF16, name="x_bf%d" % lo, align_bytes=64)[:]
+            src = picked[w][:, 0:PACK, :].rearrange("p i (s u) -> p s i u", u=4)
+            dst = x_bf.rearrange("p (s u i) -> p s i u", u=4, i=PACK)
+            cast(X_MODE[w], dst, src)
+            nc.vector.quantize_mx(out=x_codes[:, lo:hi].bitcast(FP8X4), scales=x_scales[:, lo:hi], in_=x_bf)
 
         w_scales = keep.tile([P, R // 4], I32, name="w_scales", align_bytes=64)
+        wg_codes = [keep.tile([P, BANK], I32, name="wg_codes%d" % b, align_bytes=64) for b in range(PASSES)]
+        wu_codes = [keep.tile([P, BANK // 2], I32, name="wu_codes%d" % b, align_bytes=64) for b in range(PASSES)]
 
-        def deal(dst, src, words):
+        def deal(dst, src, words, passes):
             nc.vector.tensor_copy(
-                dst.rearrange("p (t q e) -> p t q e", t=PACK, e=words),
-                src[:].rearrange("p (q t e) -> p t q e", t=PACK, e=words),
+                dst.rearrange("p (b t q e) -> p b t q e", b=passes, t=PACK, e=words),
+                src.rearrange("p (b q t e) -> p b t q e", b=passes, t=PACK, e=words),
             )
+
+        def deal_packed(b):
+            deal(wg_codes[b][:], wg_raw[b][:], 4, 1)
+            deal(wu_codes[b][:], wu_raw[b][:], 2, 1)
 
         wd_codes = keep.tile([P, PASSES, N], U32, name="wd_codes", align_bytes=64)
         wd_scales = keep.tile([P, PASSES, N], U8, name="wd_scales", align_bytes=64)
@@ -124,36 +145,35 @@ def tile_list_sigm_noneP_kernel(
                 ms = slice(64 * half, 64 * (half + 1))
                 src = wd_raw[b][:].rearrange("p t (m i) -> p m t i", i=PACK)[:, ms, :, :]
                 dst = wd_bf[:].rearrange("p i m t -> p m t i")[:, ms, :, :]
-                if W_MODE[2 * b + half] == "s":
-                    nc.scalar.copy(dst, src)
-                else:
-                    nc.vector.tensor_copy(dst, src)
+                cast(W_MODE[2 * b + half], dst, src)
             nc.vector.quantize_mx(
                 out=wd_codes[:, b, :].bitcast(FP8X4),
                 scales=wd_scales[:, b, :],
                 in_=wd_bf[:].rearrange("p i m t -> p (i m t)"),
             )
 
-        h_codes, h_scales, h_stage = {}, {}, {}
-        for lo, hi in H_PARTS:
-            codes = keep.tile([P, hi - lo, PASSES, STEP], U32, name="h_codes%d" % lo, align_bytes=64)
-            scales = keep.tile([P, hi - lo, PASSES, STEP], U8, name="h_scales%d" % lo, align_bytes=64)
-            stage = keep.tile([P, hi - lo, PASSES, STEP, PACK], BF16, name="h_bf%d" % lo, align_bytes=64)
-            for c in range(lo, hi):
-                h_codes[c], h_scales[c], h_stage[c] = codes[:, c - lo, :, :], scales[:, c - lo, :, :], stage[:, c - lo, :, :, :]
-            h_stage[lo, hi] = (codes, scales, stage)
+        h_tiles = []
+        for lo, hi in GROUPS:
+            width = STEP * (hi - lo)
+            codes = keep.tile([P, PASSES, width], U32, name="h_codes%d" % lo, align_bytes=64)
+            scales = keep.tile([P, PASSES, width], U8, name="h_scales%d" % lo, align_bytes=64)
+            stage = keep.tile([P, PASSES, width, PACK], BF16, name="h_bf%d" % lo, align_bytes=64)
+            h_tiles.append((codes, scales, stage))
 
         def hidden(c):
             cols = slice(STEP * c, STEP * (c + 1))
-            h_bf = h_stage[c]
+            g = [g for g, (lo, hi) in enumerate(GROUPS) if lo <= c < hi][0]
+            lo, hi = GROUPS[g]
+            codes, scales, stage = h_tiles[g]
+            inner = slice(STEP * (c - lo), STEP * (c - lo + 1))
             for b in range(PASSES):
-                ga = psum.tile([P, PACK, STEP], F32, name="ga")
-                ub = psum.tile([P, PACK, STEP], F32, name="ub")
+                ga = psum.tile([P, PACK, STEP], F32, name="ga", bufs=3)
+                ub = psum.tile([P, PACK, STEP], F32, name="ub", bufs=3)
                 for t in range(PACK):
-                    first = t * (R // PACK) + b * P
+                    first = b * BANK + t * P
                     nc.tensor.matmul_mx(
                         out=ga[:, t, :],
-                        lhsT=wg_codes[:, first : first + P].bitcast(FP8X4),
+                        lhsT=wg_codes[b][:, t * P : (t + 1) * P].bitcast(FP8X4),
                         lhsT_scale=w_scales[:].bitcast(U8)[4:P, first : first + P],
                         rhs=x_codes[:, cols].bitcast(FP8X4),
                         rhs_scale=x_scales[:, cols],
@@ -161,10 +181,10 @@ def tile_list_sigm_noneP_kernel(
                         stop=True,
                     )
                 for t in range(PACK):
-                    first = t * (R // PACK) + b * P
+                    first = b * BANK + t * P
                     nc.tensor.matmul_mx(
                         out=ub[:, t, :],
-                        lhsT=wu_codes.bitcast(U8)[:, 2 * first : 2 * (first + P)].bitcast(FP4X4),
+                        lhsT=wu_codes[b][:].bitcast(U8)[:, 2 * t * P : 2 * (t + 1) * P].bitcast(FP4X4),
                         lhsT_scale=w_scales[:].bitcast(U8)[:, first : first + P],
                         rhs=x_codes[:, cols].bitcast(FP8X4),
                         rhs_scale=x_scales[:, cols],
@@ -173,29 +193,34 @@ def tile_list_sigm_noneP_kernel(
                     )
                 gate = ring.tile([P, STEP, PACK], F32, name="gate")
                 nc.scalar.activation(gate[:], ga[:].rearrange("p t j -> p j t"), SIGMOID)
-                nc.vector.tensor_tensor(h_bf[:, b, :, :], ub[:].rearrange("p t j -> p j t"), gate[:], MULT)
-            for lo, hi in H_PARTS:
-                if hi == c + 1:
-                    codes, scales, stage = h_stage[lo, hi]
-                    nc.vector.quantize_mx(
-                        out=codes[:].rearrange("p c b j -> p (c b j)").bitcast(FP8X4),
-                        scales=scales[:].rearrange("p c b j -> p (c b j)"),
-                        in_=stage[:].rearrange("p c b j t -> p (c b j t)"),
-                    )
+                nc.vector.tensor_tensor(stage[:, b, inner, :], ub[:].rearrange("p t j -> p j t"), gate[:], MULT)
+            if hi == c + 1:
+                nc.vector.quantize_mx(
+                    out=codes[:].rearrange("p b j -> p (b j)").bitcast(FP8X4),
+                    scales=scales[:].rearrange("p b j -> p (b j)"),
+                    in_=stage[:].rearrange("p b j t -> p (b j t)"),
+                )
 
         y_codes = keep.tile([P, J], U32, name="y_codes", align_bytes=64)
         y_scales = keep.tile([P, J], U8, name="y_scales", align_bytes=64)
         y_rows = out_0.rearrange("(p i) j -> p i j", i=PACK)
         word_rows = out_1[0].rearrange("p j i -> p (j i)").bitcast(I32)
 
-        y_stage = {}
-        for lo, hi in Y_PARTS:
-            whole = keep.tile([P, PACK, STEP * (hi - lo)], F32, name="y%d" % lo)
-            whole_bf = keep.tile([P, STEP * (hi - lo), PACK], BF16, name="y_bf%d" % lo, align_bytes=64)
-            for c in range(lo, hi):
-                y_stage[c] = (lo, hi, whole, whole_bf)
+        y_tiles = []
+        for lo, hi in GROUPS:
+            y_tiles.append(
+                (
+                    keep.tile([P, PACK, STEP * (hi - lo)], F32, name="y%d" % lo),
+                    keep.tile([P, STEP * (hi - lo), PACK], BF16, name="y_bf%d" % lo, align_bytes=64),
+                )
+            )
 
         def output(c):
+            g = [g for g, (lo, hi) in enumerate(GROUPS) if lo <= c < hi][0]
+            lo, hi = GROUPS[g]
+            codes, scales, stage = h_tiles[g]
+            whole, whole_bf = y_tiles[g]
+            inner = slice(STEP * (c - lo), STEP * (c - lo + 1))
             acc = psum.tile([P, PACK, STEP], F32, name="acc", bufs=2)
             for i in range(PACK):
                 for b in range(PASSES):
@@ -203,56 +228,49 @@ def tile_list_sigm_noneP_kernel(
                         out=acc[:, i, :],
                         lhsT=wd_codes[:, b, P * i : P * (i + 1)].bitcast(FP8X4),
                         lhsT_scale=wd_scales[:, b, P * i : P * (i + 1)],
-                        rhs=h_codes[c][:, b, :].bitcast(FP8X4),
-                        rhs_scale=h_scales[c][:, b, :],
+                        rhs=codes[:, b, inner].bitcast(FP8X4),
+                        rhs_scale=scales[:, b, inner],
                         start=(b == 0),
                         stop=(b == PASSES - 1),
                     )
-            lo, hi, whole, whole_bf = y_stage[c]
-            inner = slice(STEP * (c - lo), STEP * (c - lo + 1))
             y = whole[:, :, inner]
             y_bf = whole_bf[:, inner, :]
-            if Y_MODE[c] == "b":
+            if Y_MODE[c] == "s":
+                nc.scalar.copy(y_bf, acc[:].rearrange("p i j -> p j i"))
                 nc.scalar.copy(y, acc[:])
-                nc.vector.tensor_copy(
+            else:
+                nc.scalar.copy(y, acc[:])
+                cast(
+                    Y_MODE[c],
                     y_bf.rearrange("p (s u) i -> p s i u", u=4),
                     y.rearrange("p i (s u) -> p s i u", u=4),
                 )
-            elif Y_MODE[c] == "v":
-                nc.vector.tensor_copy(y_bf, acc[:].rearrange("p i j -> p j i"))
-                nc.scalar.copy(y, acc[:])
-            else:
-                nc.scalar.copy(y_bf, acc[:].rearrange("p i j -> p j i"))
-                nc.scalar.copy(y, acc[:])
-            if c + 1 == hi:
-                cols = slice(STEP * lo, STEP * hi)
-                nc.sync.dma_start(y_rows[:, :, cols], whole[:])
-                nc.vector.quantize_mx(
-                    out=y_codes[:, cols].bitcast(FP8X4),
-                    scales=y_scales[:, cols],
-                    in_=whole_bf[:].rearrange("p j i -> p (j i)"),
-                )
-                nc.sync.dma_start(word_rows[:, cols], y_codes[:, cols].bitcast(I32))
+            if c + 1 < hi:
+                return
+            cols = slice(STEP * lo, STEP * hi)
+            nc.sync.dma_start(y_rows[:, :, cols], whole[:])
+            nc.vector.quantize_mx(
+                out=y_codes[:, cols].bitcast(FP8X4),
+                scales=y_scales[:, cols],
+                in_=whole_bf[:].rearrange("p j i -> p (j i)"),
+            )
+            nc.sync.dma_start(word_rows[:, cols], y_codes[:, cols].bitcast(I32))
 
-        deal(w_scales[:], scale_raw, 1)
+        deal(w_scales[:], scale_raw[:], 1, PASSES)
+        deal_packed(0)
         finish_x(0)
-        wg_codes = keep.tile([P, R], I32, name="wg_codes", align_bytes=64)[:]
-        wu_codes = keep.tile([P, R // 2], I32, name="wu_codes", align_bytes=64)[:]
-        deal(wg_codes, wg_raw, 4)
-        deal(wu_codes, wu_raw, 2)
         finish_x(1)
+        deal_packed(1)
         hidden(0)
-        hidden(1)
-        finish_x(2)
-        hidden(2)
         quantize_wd(0)
         quantize_wd(1)
-        finish_x(3)
-        hidden(3)
-        for c in range(4, J // STEP):
+        for c in range(1, J // STEP):
             hidden(c)
-            output(c - 4)
-        for c in range(J // STEP - 4, J // STEP):
+            if c + 1 < len(X_PARTS):
+                finish_x(c + 1)
+            if c >= 2:
+                output(c - 2)
+        for c in range(J // STEP - 2, J // STEP):
             output(c)
 
         for quad in range(4):

@@ -25,7 +25,6 @@ HEAD = 256
 PASSES = R // (P * PACK)
 X_PARTS = [(0, 256), (256, 512), (512, 768), (768, 1024)]
 GROUPS = [(0, 2), (2, 4), (4, 5), (5, 6), (6, 7), (7, 8)]
-X_REUSE = {0: 3}
 X_MODE = "ssss"
 W_MODE = "vvvv"
 Y_MODE = "ssssvvvv"
@@ -40,6 +39,14 @@ def tile_list_sigm_noneP_kernel(
         ring = ctx.enter_context(tc.tile_pool(name="ring", bufs=8))
         psum = ctx.enter_context(tc.psum_pool(name="psum", bufs=1))
 
+        def cast(mode, dst, src):
+            if mode == "s":
+                nc.scalar.copy(dst, src)
+            elif mode == "g":
+                nc.gpsimd.tensor_scalar(dst, src, 1.0, 0.0, MULT, ADD)
+            else:
+                nc.vector.tensor_copy(dst, src)
+
         offsets = keep.tile([P, J // 16], U16, name="offsets")
         scale_raw = keep.tile([P, R // 4], I32, name="scale_raw")
         nc.vector.memset(scale_raw[:], 0)
@@ -51,7 +58,8 @@ def tile_list_sigm_noneP_kernel(
 
         x_rows = xT.rearrange("(p i) t -> i p t", i=PACK)
         x_plane = [keep.tile([P, T], F32, name="x_plane%d" % i) for i in range(PACK)]
-        weight = keep.tile([P, J], F32, name="weight")
+        weight = keep.tile([P, J], F32, name="weight", align_bytes=64)
+        w_piece = keep.tile([P, 64], F32, name="w_piece", align_bytes=64)
         wg_raw = [keep.tile([P, BANK], I32, name="wg_raw%d" % b) for b in range(PASSES)]
         wu_raw = [keep.tile([P, BANK // 2], I32, name="wu_raw%d" % b) for b in range(PASSES)]
         wd_raw = [keep.tile([P, PACK, N], F32, name="wd_raw%d" % b) for b in range(PASSES)]
@@ -70,10 +78,9 @@ def tile_list_sigm_noneP_kernel(
             for t in range(PACK):
                 nc.sync.dma_start(wd_raw[b][:, t, :], rows[t])
 
+        nc.sync.dma_start(w_piece[:], wgt.rearrange("(g r) (a b) -> g (r a) b", r=16, b=64)[:, ::17, :])
         load_x(0)
         nc.sync.dma_start(offsets[:], offs)
-        nc.sync.dma_start(weight[:, 0:HEAD], wgt[:, 0:HEAD])
-        nc.sync.dma_start(weight[:, HEAD:J], wgt[:, HEAD:J])
         load_x(1)
         load_scales(nc.sync, wu_scales, 0)
         load_x(2)
@@ -88,36 +95,39 @@ def tile_list_sigm_noneP_kernel(
         warm_out = keep.tile([P, 1], F32, name="warm_out")
         nc.vector.memset(warm[:], 0.0)
         nc.scalar.activation(warm_out[:], warm[:], SIGMOID)
+        turned = keep.tile([P, 2, 32], F32, name="turned", align_bytes=64)
+        for k in range(2):
+            nc.vector.transpose(turned[:, k, :], w_piece[:, 32 * k : 32 * (k + 1)])
+        spread = keep.tile([P, J], F32, name="spread", align_bytes=64)
+        for half in range(2):
+            rs = slice(8 * half, 8 * (half + 1))
+            cols = slice(J // 2 * half, J // 2 * (half + 1))
+            src = turned[:].rearrange("p k (h r) -> p r (k h)", h=2)[:, rs, :].unsqueeze(3).broadcast_to([P, 8, 4, 16])
+            dst = spread[:, cols].rearrange("p (r c e) -> p r c e", r=8, c=4)
+            cast("vs"[half], dst, src)
+            nc.vector.transpose(weight[:, cols], spread[:, cols])
 
-        def cast(mode, dst, src):
-            if mode == "s":
-                nc.scalar.copy(dst, src)
-            elif mode == "g":
-                nc.gpsimd.tensor_scalar(dst, src, 1.0, 0.0, MULT, ADD)
-            else:
-                nc.vector.tensor_copy(dst, src)
 
-        picked = [keep.tile([P, PACK + 1, hi - lo], F32, name="picked%d" % lo, align_bytes=64) for lo, hi in X_PARTS]
+        picked_flat = keep.tile([P, PACK * J + HEAD], F32, name="picked", align_bytes=64)
+        picked = picked_flat[:, 0 : PACK * J].rearrange("p (i j) -> p i j", i=PACK)
         x_codes = keep.tile([P, J], U32, name="x_codes", align_bytes=64)
         x_scales = keep.tile([P, J], U8, name="x_scales", align_bytes=64)
 
-        def gather(i, w):
-            lo, hi = X_PARTS[w]
+        def gather(i, lo, hi):
             window = x_plane[i][:].indirect(offsets[:, lo // 16 : hi // 16])
-            nc.vector.tensor_tensor(picked[w][:, i, :], window, weight[:, lo:hi], MULT)
+            nc.vector.tensor_tensor(picked[:, i, lo:hi], window, weight[:, lo:hi], MULT)
 
         for i in range(PACK - 1):
-            for w in range(len(X_PARTS)):
-                gather(i, w)
+            gather(i, 0, J)
 
         def finish_x(w):
             lo, hi = X_PARTS[w]
-            gather(PACK - 1, w)
-            if w in X_REUSE:
-                x_bf = picked[X_REUSE[w]][:, PACK - 1 :, :].rearrange("p a j -> p (a j)")[:, 0 : 2 * (hi - lo)].bitcast(BF16)
+            gather(PACK - 1, lo, hi)
+            if w == 0:
+                x_bf = picked_flat[:, PACK * J - HEAD : PACK * J + HEAD].bitcast(BF16)
             else:
                 x_bf = keep.tile([P, PACK * (hi - lo)], BF16, name="x_bf%d" % lo, align_bytes=64)[:]
-            src = picked[w][:, 0:PACK, :].rearrange("p i (s u) -> p s i u", u=4)
+            src = picked[:, :, lo:hi].rearrange("p i (s u) -> p s i u", u=4)
             dst = x_bf.rearrange("p (s u i) -> p s i u", u=4, i=PACK)
             cast(X_MODE[w], dst, src)
             nc.vector.quantize_mx(out=x_codes[:, lo:hi].bitcast(FP8X4), scales=x_scales[:, lo:hi], in_=x_bf)

@@ -25,8 +25,8 @@ HEAD = 256
 PASSES = R // (P * PACK)
 X_PARTS = [(0, 256), (256, 512), (512, 768), (768, 1024)]
 GROUPS = [(0, 2), (2, 4), (4, 5), (5, 6), (6, 7), (7, 8)]
-X_MODE = "ssss"
-W_MODE = "vvvv"
+X_MODE = "sssv"
+W_MODE = "svvv"
 Y_MODE = "ssssvvvv"
 
 
@@ -204,7 +204,13 @@ def tile_list_sigm_noneP_kernel(
                 gate = ring.tile([P, STEP, PACK], F32, name="gate")
                 nc.scalar.activation(gate[:], ga[:].rearrange("p t j -> p j t"), SIGMOID)
                 nc.vector.tensor_tensor(stage[:, b, inner, :], ub[:].rearrange("p t j -> p j t"), gate[:], MULT)
-            if hi == c + 1:
+                if c == J // STEP - 1:
+                    nc.vector.quantize_mx(
+                        out=codes[:, b, :].bitcast(FP8X4),
+                        scales=scales[:, b, :],
+                        in_=stage[:, b, :, :].rearrange("p j t -> p (j t)"),
+                    )
+            if hi == c + 1 and c < J // STEP - 1:
                 nc.vector.quantize_mx(
                     out=codes[:].rearrange("p b j -> p (b j)").bitcast(FP8X4),
                     scales=scales[:].rearrange("p b j -> p (b j)"),
@@ -216,53 +222,50 @@ def tile_list_sigm_noneP_kernel(
         y_rows = out_0.rearrange("(p i) j -> p i j", i=PACK)
         word_rows = out_1[0].rearrange("p j i -> p (j i)").bitcast(I32)
 
-        y_tiles = []
-        for lo, hi in GROUPS:
-            y_tiles.append(
-                (
-                    keep.tile([P, PACK, STEP * (hi - lo)], F32, name="y%d" % lo),
-                    keep.tile([P, STEP * (hi - lo), PACK], BF16, name="y_bf%d" % lo, align_bytes=64),
-                )
-            )
-
-        def output(c):
-            g = [g for g, (lo, hi) in enumerate(GROUPS) if lo <= c < hi][0]
+        def output(g):
             lo, hi = GROUPS[g]
-            codes, scales, stage = h_tiles[g]
-            whole, whole_bf = y_tiles[g]
-            inner = slice(STEP * (c - lo), STEP * (c - lo + 1))
-            acc = psum.tile([P, PACK, STEP], F32, name="acc", bufs=2)
-            for i in range(PACK):
-                for b in range(PASSES):
-                    nc.tensor.matmul_mx(
-                        out=acc[:, i, :],
-                        lhsT=wd_codes[:, b, P * i : P * (i + 1)].bitcast(FP8X4),
-                        lhsT_scale=wd_scales[:, b, P * i : P * (i + 1)],
-                        rhs=codes[:, b, inner].bitcast(FP8X4),
-                        rhs_scale=scales[:, b, inner],
-                        start=(b == 0),
-                        stop=(b == PASSES - 1),
-                    )
-            y = whole[:, :, inner]
-            y_bf = whole_bf[:, inner, :]
-            if Y_MODE[c] == "s":
-                nc.scalar.copy(y_bf, acc[:].rearrange("p i j -> p j i"))
-                nc.scalar.copy(y, acc[:])
-            else:
-                nc.scalar.copy(y, acc[:])
-                cast(
-                    Y_MODE[c],
-                    y_bf.rearrange("p (s u) i -> p s i u", u=4),
-                    y.rearrange("p i (s u) -> p s i u", u=4),
-                )
-            if c + 1 < hi:
-                return
+            width = STEP * (hi - lo)
             cols = slice(STEP * lo, STEP * hi)
-            nc.sync.dma_start(y_rows[:, :, cols], whole[:])
+            last = g == len(GROUPS) - 1
+            codes, scales, stage = h_tiles[g]
+            y = keep.tile([P, PACK, width], F32, name="y%d" % lo)
+            y_bf = keep.tile([P, width, PACK], BF16, name="y_bf%d" % lo, align_bytes=64)
+            per_bank = 2 if last else BANK // width
+            banks = [psum.tile([P, per_bank, width], F32, name="acc", bufs=2) for i0 in range(0, PACK, per_bank)]
+
+            def product(i, b, start, stop):
+                nc.tensor.matmul_mx(
+                    out=banks[i // per_bank][:, i % per_bank, :],
+                    lhsT=wd_codes[:, b, P * i : P * (i + 1)].bitcast(FP8X4),
+                    lhsT_scale=wd_scales[:, b, P * i : P * (i + 1)],
+                    rhs=codes[:, b, :].bitcast(FP8X4),
+                    rhs_scale=scales[:, b, :],
+                    start=start,
+                    stop=stop,
+                )
+
+            if last:
+                for b in range(PASSES):
+                    for i in range(PACK):
+                        product(i, b, b == 0 and i % 2 == 0, b == PASSES - 1 and i % 2 == 1)
+                nc.scalar.copy(y[:, 0:2, :], banks[0][:])
+                nc.vector.tensor_copy(y[:, 2:4, :], banks[1][:])
+            else:
+                for k, bank in enumerate(banks):
+                    for i in range(k * per_bank, (k + 1) * per_bank):
+                        for b in range(PASSES):
+                            product(i, b, b == 0, b == PASSES - 1)
+                    nc.scalar.copy(y[:, k * per_bank : (k + 1) * per_bank, :], bank[:])
+            nc.sync.dma_start(y_rows[:, :, cols], y[:])
+            cast(
+                "s" if g < 2 else "v",
+                y_bf[:].rearrange("p (s u) i -> p s i u", u=4),
+                y[:].rearrange("p i (s u) -> p s i u", u=4),
+            )
             nc.vector.quantize_mx(
                 out=y_codes[:, cols].bitcast(FP8X4),
                 scales=y_scales[:, cols],
-                in_=whole_bf[:].rearrange("p j i -> p (j i)"),
+                in_=y_bf[:].rearrange("p j i -> p (j i)"),
             )
             nc.sync.dma_start(word_rows[:, cols], y_codes[:, cols].bitcast(I32))
 
@@ -274,14 +277,21 @@ def tile_list_sigm_noneP_kernel(
         hidden(0)
         quantize_wd(0)
         quantize_wd(1)
-        for c in range(1, J // STEP):
-            hidden(c)
-            if c + 1 < len(X_PARTS):
-                finish_x(c + 1)
-            if c >= 2:
-                output(c - 2)
-        for c in range(J // STEP - 2, J // STEP):
-            output(c)
+        hidden(1)
+        finish_x(2)
+        hidden(2)
+        finish_x(3)
+        output(0)
+        hidden(3)
+        hidden(4)
+        output(1)
+        hidden(5)
+        hidden(6)
+        output(2)
+        hidden(7)
+        output(3)
+        output(4)
+        output(5)
 
         for quad in range(4):
             queue = nc.scalar if quad % 2 else nc.sync

@@ -74,7 +74,7 @@ def tile_list_sigm_noneP_kernel(
             nc.sync.dma_start(wu_raw[b][:], wu_hbm[:, 256 * b : 256 * (b + 1)])
 
         def load_wd(b):
-            rows = wd[512 * b : 512 * (b + 1), :].rearrange("(q t e) n -> t q e n", t=PACK, e=4)
+            rows = wd[512 * b : 512 * (b + 1), :].rearrange("(q t e) n -> t q e n", t=PACK, e=8)
             for t in range(PACK):
                 nc.sync.dma_start(wd_raw[b][:, t, :], rows[t])
 
@@ -122,7 +122,8 @@ def tile_list_sigm_noneP_kernel(
 
         def finish_x(w):
             lo, hi = X_PARTS[w]
-            gather(PACK - 1, lo, hi)
+            if w != 2:
+                gather(PACK - 1, lo, hi + HEAD if w == 1 else hi)
             if w == 0:
                 x_bf = picked_flat[:, PACK * J - HEAD : PACK * J + HEAD].bitcast(BF16)
             else:
@@ -143,8 +144,8 @@ def tile_list_sigm_noneP_kernel(
             )
 
         def deal_packed(b):
-            deal(wg_codes[b][:], wg_raw[b][:], 4, 1)
-            deal(wu_codes[b][:], wu_raw[b][:], 2, 1)
+            deal(wg_codes[b][:], wg_raw[b][:], 8, 1)
+            deal(wu_codes[b][:], wu_raw[b][:], 4, 1)
 
         wd_codes = keep.tile([P, PASSES, N], U32, name="wd_codes", align_bytes=64)
         wd_scales = keep.tile([P, PASSES, N], U8, name="wd_scales", align_bytes=64)
@@ -231,7 +232,7 @@ def tile_list_sigm_noneP_kernel(
             y = keep.tile([P, PACK, width], F32, name="y%d" % lo)
             y_bf = keep.tile([P, width, PACK], BF16, name="y_bf%d" % lo, align_bytes=64)
             per_bank = 2 if last else BANK // width
-            banks = [psum.tile([P, per_bank, width], F32, name="acc", bufs=2) for i0 in range(0, PACK, per_bank)]
+            banks = [psum.tile([P, per_bank, width], F32, name="ga" if last else "acc", bufs=3 if last else 2) for i0 in range(0, PACK, per_bank)]
 
             def product(i, b, start, stop):
                 nc.tensor.matmul_mx(
@@ -269,7 +270,7 @@ def tile_list_sigm_noneP_kernel(
             )
             nc.sync.dma_start(word_rows[:, cols], y_codes[:, cols].bitcast(I32))
 
-        deal(w_scales[:], scale_raw[:], 1, PASSES)
+        deal(w_scales[:], scale_raw[:], 2, PASSES)
         deal_packed(0)
         finish_x(0)
         finish_x(1)

@@ -268,7 +268,9 @@ def tile_list_sigm_noneP_kernel(
                 scales=y_scales[:, cols],
                 in_=y_bf[:].rearrange("p j i -> p (j i)"),
             )
-            nc.sync.dma_start(word_rows[:, cols], y_codes[:, cols].bitcast(I32))
+            if g not in (2, 3):
+                words = slice(STEP * GROUPS[2][0], STEP * hi) if g == 4 else cols
+                nc.sync.dma_start(word_rows[:, words], y_codes[:, words].bitcast(I32))
 
         deal(w_scales[:], scale_raw[:], 2, PASSES)
         deal_packed(0)

@@ -14,20 +14,24 @@ U8 = mybir.dt.uint8
 FP8X4 = mybir.dt.float8_e4m3fn_x4
 FP4X4 = mybir.dt.float4_e2m1fn_x4
 MULT = mybir.AluOpType.mult
-ADD = mybir.AluOpType.add
 SIGMOID = mybir.ActivationFunctionType.Sigmoid
 
 P = 128
 PACK = 4
-STEP = 128
+RUN = 8
+PASS_ROWS = P * PACK
+PASSES = R // PASS_ROWS
 BANK = 512
-HEAD = 256
-PASSES = R // (P * PACK)
-X_PARTS = [(0, 256), (256, 512), (512, 768), (768, 1024)]
+CHUNK = BANK // PACK
+CHUNKS = J // CHUNK
+PART = 2 * CHUNK
+PARTS = J // PART
 GROUPS = [(0, 2), (2, 4), (4, 5), (5, 6), (6, 7), (7, 8)]
-X_MODE = "sssv"
-W_MODE = "svvv"
-Y_MODE = "ssssvvvv"
+LAG = 3
+GATE_BUFS = 8
+STAGE_BANKS = 3
+WARM_PASSES = 4
+OUT_BANKS = 2
 
 
 def tile_list_sigm_noneP_kernel(
@@ -36,79 +40,70 @@ def tile_list_sigm_noneP_kernel(
     nc = tc.nc
     with ExitStack() as ctx:
         keep = ctx.enter_context(tc.tile_pool(name="keep", bufs=1))
-        ring = ctx.enter_context(tc.tile_pool(name="ring", bufs=8))
+        ring = ctx.enter_context(tc.tile_pool(name="ring", bufs=GATE_BUFS))
         psum = ctx.enter_context(tc.psum_pool(name="psum", bufs=1))
 
-        def cast(mode, dst, src):
-            if mode == "s":
+        def copy(on_scalar, dst, src):
+            if on_scalar:
                 nc.scalar.copy(dst, src)
-            elif mode == "g":
-                nc.gpsimd.tensor_scalar(dst, src, 1.0, 0.0, MULT, ADD)
             else:
                 nc.vector.tensor_copy(dst, src)
+
+        def quantize(codes, scales, values):
+            nc.vector.quantize_mx(out=codes.bitcast(FP8X4), scales=scales, in_=values)
 
         offsets = keep.tile([P, J // 16], U16, name="offsets")
         scale_raw = keep.tile([P, R // 4], I32, name="scale_raw")
         nc.vector.memset(scale_raw[:], 0)
 
-        def load_scales(queue, source, first_row):
+        def load_scales(source, first_row):
             for quad in range(4):
                 rows = slice(32 * quad + first_row, 32 * quad + first_row + 4)
-                queue.dma_start(scale_raw[rows, :], source[0, 4 * quad : 4 * quad + 4, :].bitcast(I32))
+                nc.sync.dma_start(scale_raw[rows, :], source[0, 4 * quad : 4 * quad + 4, :].bitcast(I32))
 
         x_rows = xT.rearrange("(p i) t -> i p t", i=PACK)
         x_plane = [keep.tile([P, T], F32, name="x_plane%d" % i) for i in range(PACK)]
         weight = keep.tile([P, J], F32, name="weight", align_bytes=64)
-        w_piece = keep.tile([P, 64], F32, name="w_piece", align_bytes=64)
-        wg_raw = [keep.tile([P, BANK], I32, name="wg_raw%d" % b) for b in range(PASSES)]
-        wu_raw = [keep.tile([P, BANK // 2], I32, name="wu_raw%d" % b) for b in range(PASSES)]
+        w_piece = keep.tile([P, J // 16], F32, name="w_piece", align_bytes=64)
+        wg_raw = [keep.tile([P, PASS_ROWS], I32, name="wg_raw%d" % b, align_bytes=64) for b in range(PASSES)]
+        wu_raw = [keep.tile([P, PASS_ROWS // 2], I32, name="wu_raw%d" % b) for b in range(PASSES)]
         wd_raw = [keep.tile([P, PACK, N], F32, name="wd_raw%d" % b) for b in range(PASSES)]
         wg_hbm = wg_words[0].rearrange("p r i -> p (r i)").bitcast(I32)
         wu_hbm = wu_words[0].bitcast(I32)
 
-        def load_x(i):
-            nc.sync.dma_start(x_plane[i][:], x_rows[i])
-
-        def load_packed(b):
-            nc.sync.dma_start(wg_raw[b][:], wg_hbm[:, 512 * b : 512 * (b + 1)])
-            nc.sync.dma_start(wu_raw[b][:], wu_hbm[:, 256 * b : 256 * (b + 1)])
-
-        def load_wd(b):
-            rows = wd[512 * b : 512 * (b + 1), :].rearrange("(q t e) n -> t q e n", t=PACK, e=8)
+        nc.sync.dma_start(w_piece[:], wgt.rearrange("(g r) (a b) -> g (r a) b", r=16, b=64)[:, ::17, :])
+        nc.sync.dma_start(x_plane[0][:], x_rows[0])
+        nc.sync.dma_start(offsets[:], offs)
+        nc.sync.dma_start(x_plane[1][:], x_rows[1])
+        load_scales(wu_scales, 0)
+        nc.sync.dma_start(x_plane[2][:], x_rows[2])
+        load_scales(wg_scales, 4)
+        nc.sync.dma_start(x_plane[3][:], x_rows[3])
+        for b in range(PASSES):
+            nc.sync.dma_start(wg_raw[b][:], wg_hbm[:, PASS_ROWS * b : PASS_ROWS * (b + 1)])
+            nc.sync.dma_start(wu_raw[b][:], wu_hbm[:, PASS_ROWS // 2 * b : PASS_ROWS // 2 * (b + 1)])
+        for b in range(PASSES):
+            rows = wd[PASS_ROWS * b : PASS_ROWS * (b + 1), :].rearrange("(q t e) n -> t q e n", t=PACK, e=RUN)
             for t in range(PACK):
                 nc.sync.dma_start(wd_raw[b][:, t, :], rows[t])
-
-        nc.sync.dma_start(w_piece[:], wgt.rearrange("(g r) (a b) -> g (r a) b", r=16, b=64)[:, ::17, :])
-        load_x(0)
-        nc.sync.dma_start(offsets[:], offs)
-        load_x(1)
-        load_scales(nc.sync, wu_scales, 0)
-        load_x(2)
-        load_scales(nc.sync, wg_scales, 4)
-        load_x(3)
-        load_packed(0)
-        load_packed(1)
-        load_wd(0)
-        load_wd(1)
 
         warm = keep.tile([P, 1], F32, name="warm")
         warm_out = keep.tile([P, 1], F32, name="warm_out")
         nc.vector.memset(warm[:], 0.0)
         nc.scalar.activation(warm_out[:], warm[:], SIGMOID)
+
         turned = keep.tile([P, 2, 32], F32, name="turned", align_bytes=64)
-        for k in range(2):
-            nc.vector.transpose(turned[:, k, :], w_piece[:, 32 * k : 32 * (k + 1)])
+        for s in range(2):
+            nc.vector.transpose(turned[:, s, :], w_piece[:, 32 * s : 32 * (s + 1)])
         spread = keep.tile([P, J], F32, name="spread", align_bytes=64)
         for half in range(2):
-            rs = slice(8 * half, 8 * (half + 1))
             cols = slice(J // 2 * half, J // 2 * (half + 1))
-            src = turned[:].rearrange("p k (h r) -> p r (k h)", h=2)[:, rs, :].unsqueeze(3).broadcast_to([P, 8, 4, 16])
+            src = turned[:].rearrange("p s (h r) -> p r (s h)", h=2)[:, 8 * half : 8 * (half + 1), :]
             dst = spread[:, cols].rearrange("p (r c e) -> p r c e", r=8, c=4)
-            cast("vs"[half], dst, src)
+            copy(half == 1, dst, src.unsqueeze(3).broadcast_to([P, 8, 4, 16]))
             nc.vector.transpose(weight[:, cols], spread[:, cols])
 
-
-        picked_flat = keep.tile([P, PACK * J + HEAD], F32, name="picked", align_bytes=64)
+        picked_flat = keep.tile([P, PACK * J + PART], F32, name="picked", align_bytes=64)
         picked = picked_flat[:, 0 : PACK * J].rearrange("p (i j) -> p i j", i=PACK)
         x_codes = keep.tile([P, J], U32, name="x_codes", align_bytes=64)
         x_scales = keep.tile([P, J], U8, name="x_scales", align_bytes=64)
@@ -120,32 +115,30 @@ def tile_list_sigm_noneP_kernel(
         for i in range(PACK - 1):
             gather(i, 0, J)
 
-        def finish_x(w):
-            lo, hi = X_PARTS[w]
-            if w != 2:
-                gather(PACK - 1, lo, hi + HEAD if w == 1 else hi)
-            if w == 0:
-                x_bf = picked_flat[:, PACK * J - HEAD : PACK * J + HEAD].bitcast(BF16)
-            else:
-                x_bf = keep.tile([P, PACK * (hi - lo)], BF16, name="x_bf%d" % lo, align_bytes=64)[:]
-            src = picked[:, :, lo:hi].rearrange("p i (s u) -> p s i u", u=4)
+        def finish_x(part, x_bf):
+            cols = slice(PART * part, PART * (part + 1))
+            src = picked[:, :, cols].rearrange("p i (s u) -> p s i u", u=4)
             dst = x_bf.rearrange("p (s u i) -> p s i u", u=4, i=PACK)
-            cast(X_MODE[w], dst, src)
-            nc.vector.quantize_mx(out=x_codes[:, lo:hi].bitcast(FP8X4), scales=x_scales[:, lo:hi], in_=x_bf)
+            copy(part < PARTS - 1, dst, src)
+            quantize(x_codes[:, cols], x_scales[:, cols], x_bf)
+
+        def x_stage(part):
+            return keep.tile([P, PACK * PART], BF16, name="x_bf%d" % (PART * part), align_bytes=64)[:]
 
         w_scales = keep.tile([P, R // 4], I32, name="w_scales", align_bytes=64)
-        wg_codes = [keep.tile([P, BANK], I32, name="wg_codes%d" % b, align_bytes=64) for b in range(PASSES)]
-        wu_codes = [keep.tile([P, BANK // 2], I32, name="wu_codes%d" % b, align_bytes=64) for b in range(PASSES)]
+        wg_codes = [keep.tile([P, PASS_ROWS], I32, name="wg_codes%d" % b, align_bytes=64) for b in range(PASSES)]
+        wu_codes = [keep.tile([P, PASS_ROWS // 2], I32, name="wu_codes%d" % b, align_bytes=64) for b in range(PASSES)]
 
-        def deal(dst, src, words, passes):
+        def reorder(dst, src, column_bytes, passes):
+            run = RUN * column_bytes // 4
             nc.vector.tensor_copy(
-                dst.rearrange("p (b t q e) -> p b t q e", b=passes, t=PACK, e=words),
-                src.rearrange("p (b q t e) -> p b t q e", b=passes, t=PACK, e=words),
+                dst.rearrange("p (b t q e) -> p b t q e", b=passes, t=PACK, e=run),
+                src.rearrange("p (b q t e) -> p b t q e", b=passes, t=PACK, e=run),
             )
 
-        def deal_packed(b):
-            deal(wg_codes[b][:], wg_raw[b][:], 8, 1)
-            deal(wu_codes[b][:], wu_raw[b][:], 4, 1)
+        def reorder_packed(b):
+            reorder(wg_codes[b][:], wg_raw[b][:], 4, 1)
+            reorder(wu_codes[b][:], wu_raw[b][:], 2, 1)
 
         wd_codes = keep.tile([P, PASSES, N], U32, name="wd_codes", align_bytes=64)
         wd_scales = keep.tile([P, PASSES, N], U8, name="wd_scales", align_bytes=64)
@@ -153,35 +146,32 @@ def tile_list_sigm_noneP_kernel(
         def quantize_wd(b):
             wd_bf = keep.tile([P, PACK, P, PACK], BF16, name="wd_bf%d" % b, align_bytes=64)
             for half in range(2):
-                ms = slice(64 * half, 64 * (half + 1))
+                ms = slice(P // 2 * half, P // 2 * (half + 1))
                 src = wd_raw[b][:].rearrange("p t (m i) -> p m t i", i=PACK)[:, ms, :, :]
                 dst = wd_bf[:].rearrange("p i m t -> p m t i")[:, ms, :, :]
-                cast(W_MODE[2 * b + half], dst, src)
-            nc.vector.quantize_mx(
-                out=wd_codes[:, b, :].bitcast(FP8X4),
-                scales=wd_scales[:, b, :],
-                in_=wd_bf[:].rearrange("p i m t -> p (i m t)"),
-            )
+                copy(b == 0 and half == 0, dst, src)
+            quantize(wd_codes[:, b, :], wd_scales[:, b, :], wd_bf[:].rearrange("p i m t -> p (i m t)"))
 
         h_tiles = []
         for lo, hi in GROUPS:
-            width = STEP * (hi - lo)
+            width = CHUNK * (hi - lo)
             codes = keep.tile([P, PASSES, width], U32, name="h_codes%d" % lo, align_bytes=64)
             scales = keep.tile([P, PASSES, width], U8, name="h_scales%d" % lo, align_bytes=64)
-            stage = keep.tile([P, PASSES, width, PACK], BF16, name="h_bf%d" % lo, align_bytes=64)
-            h_tiles.append((codes, scales, stage))
+            h_bf = keep.tile([P, PASSES, width, PACK], BF16, name="h_bf%d" % lo, align_bytes=64)
+            h_tiles.append((codes, scales, h_bf))
 
         def hidden(c):
-            cols = slice(STEP * c, STEP * (c + 1))
+            cols = slice(CHUNK * c, CHUNK * (c + 1))
             g = [g for g, (lo, hi) in enumerate(GROUPS) if lo <= c < hi][0]
             lo, hi = GROUPS[g]
-            codes, scales, stage = h_tiles[g]
-            inner = slice(STEP * (c - lo), STEP * (c - lo + 1))
+            codes, scales, h_bf = h_tiles[g]
+            inner = slice(CHUNK * (c - lo), CHUNK * (c - lo + 1))
+            last = c == CHUNKS - 1
             for b in range(PASSES):
-                ga = psum.tile([P, PACK, STEP], F32, name="ga", bufs=3)
-                ub = psum.tile([P, PACK, STEP], F32, name="ub", bufs=3)
+                ga = psum.tile([P, PACK, CHUNK], F32, name="ga", bufs=STAGE_BANKS)
+                ub = psum.tile([P, PACK, CHUNK], F32, name="ub", bufs=STAGE_BANKS)
                 for t in range(PACK):
-                    first = b * BANK + t * P
+                    first = b * PASS_ROWS + t * P
                     nc.tensor.matmul_mx(
                         out=ga[:, t, :],
                         lhsT=wg_codes[b][:, t * P : (t + 1) * P].bitcast(FP8X4),
@@ -192,7 +182,7 @@ def tile_list_sigm_noneP_kernel(
                         stop=True,
                     )
                 for t in range(PACK):
-                    first = b * BANK + t * P
+                    first = b * PASS_ROWS + t * P
                     nc.tensor.matmul_mx(
                         out=ub[:, t, :],
                         lhsT=wu_codes[b][:].bitcast(U8)[:, 2 * t * P : 2 * (t + 1) * P].bitcast(FP4X4),
@@ -202,37 +192,35 @@ def tile_list_sigm_noneP_kernel(
                         start=True,
                         stop=True,
                     )
-                gate = ring.tile([P, STEP, PACK], F32, name="gate")
+                gate = ring.tile([P, CHUNK, PACK], F32, name="gate")
                 nc.scalar.activation(gate[:], ga[:].rearrange("p t j -> p j t"), SIGMOID)
-                nc.vector.tensor_tensor(stage[:, b, inner, :], ub[:].rearrange("p t j -> p j t"), gate[:], MULT)
-                if c == J // STEP - 1:
-                    nc.vector.quantize_mx(
-                        out=codes[:, b, :].bitcast(FP8X4),
-                        scales=scales[:, b, :],
-                        in_=stage[:, b, :, :].rearrange("p j t -> p (j t)"),
-                    )
-            if hi == c + 1 and c < J // STEP - 1:
-                nc.vector.quantize_mx(
-                    out=codes[:].rearrange("p b j -> p (b j)").bitcast(FP8X4),
-                    scales=scales[:].rearrange("p b j -> p (b j)"),
-                    in_=stage[:].rearrange("p b j t -> p (b j t)"),
+                nc.vector.tensor_tensor(h_bf[:, b, inner, :], ub[:].rearrange("p t j -> p j t"), gate[:], MULT)
+                if last:
+                    quantize(codes[:, b, :], scales[:, b, :], h_bf[:, b, :, :].rearrange("p j t -> p (j t)"))
+            if hi == c + 1 and not last:
+                quantize(
+                    codes[:].rearrange("p b j -> p (b j)"),
+                    scales[:].rearrange("p b j -> p (b j)"),
+                    h_bf[:].rearrange("p b j t -> p (b j t)"),
                 )
 
         y_codes = keep.tile([P, J], U32, name="y_codes", align_bytes=64)
         y_scales = keep.tile([P, J], U8, name="y_scales", align_bytes=64)
         y_rows = out_0.rearrange("(p i) j -> p i j", i=PACK)
         word_rows = out_1[0].rearrange("p j i -> p (j i)").bitcast(I32)
+        first_single = [lo for lo, hi in GROUPS if hi - lo == 1][0]
 
         def output(g):
             lo, hi = GROUPS[g]
-            width = STEP * (hi - lo)
-            cols = slice(STEP * lo, STEP * hi)
-            last = g == len(GROUPS) - 1
-            codes, scales, stage = h_tiles[g]
+            width = CHUNK * (hi - lo)
+            cols = slice(CHUNK * lo, CHUNK * hi)
+            last = hi == CHUNKS
+            codes, scales, h_bf = h_tiles[g]
             y = keep.tile([P, PACK, width], F32, name="y%d" % lo)
             y_bf = keep.tile([P, width, PACK], BF16, name="y_bf%d" % lo, align_bytes=64)
-            per_bank = 2 if last else BANK // width
-            banks = [psum.tile([P, per_bank, width], F32, name="ga" if last else "acc", bufs=3 if last else 2) for i0 in range(0, PACK, per_bank)]
+            per_bank = PACK // 2 if last else BANK // width
+            tag, bufs = ("ga", STAGE_BANKS) if last else ("acc", OUT_BANKS)
+            banks = [psum.tile([P, per_bank, width], F32, name=tag, bufs=bufs) for slot in range(PACK // per_bank)]
 
             def product(i, b, start, stop):
                 nc.tensor.matmul_mx(
@@ -248,53 +236,62 @@ def tile_list_sigm_noneP_kernel(
             if last:
                 for b in range(PASSES):
                     for i in range(PACK):
-                        product(i, b, b == 0 and i % 2 == 0, b == PASSES - 1 and i % 2 == 1)
-                nc.scalar.copy(y[:, 0:2, :], banks[0][:])
-                nc.vector.tensor_copy(y[:, 2:4, :], banks[1][:])
+                        product(i, b, b == 0 and i % per_bank == 0, b == PASSES - 1 and i % per_bank == per_bank - 1)
+                for slot, bank in enumerate(banks):
+                    copy(slot == 0, y[:, slot * per_bank : (slot + 1) * per_bank, :], bank[:])
             else:
-                for k, bank in enumerate(banks):
-                    for i in range(k * per_bank, (k + 1) * per_bank):
+                for slot, bank in enumerate(banks):
+                    for i in range(slot * per_bank, (slot + 1) * per_bank):
                         for b in range(PASSES):
                             product(i, b, b == 0, b == PASSES - 1)
-                    nc.scalar.copy(y[:, k * per_bank : (k + 1) * per_bank, :], bank[:])
+                    nc.scalar.copy(y[:, slot * per_bank : (slot + 1) * per_bank, :], bank[:])
             nc.sync.dma_start(y_rows[:, :, cols], y[:])
-            cast(
-                "s" if g < 2 else "v",
+            copy(
+                hi - lo > 1,
                 y_bf[:].rearrange("p (s u) i -> p s i u", u=4),
                 y[:].rearrange("p i (s u) -> p s i u", u=4),
             )
-            nc.vector.quantize_mx(
-                out=y_codes[:, cols].bitcast(FP8X4),
-                scales=y_scales[:, cols],
-                in_=y_bf[:].rearrange("p j i -> p (j i)"),
-            )
-            if g not in (2, 3):
-                words = slice(STEP * GROUPS[2][0], STEP * hi) if g == 4 else cols
-                nc.sync.dma_start(word_rows[:, words], y_codes[:, words].bitcast(I32))
+            quantize(y_codes[:, cols], y_scales[:, cols], y_bf[:].rearrange("p j i -> p (j i)"))
+            if hi - lo > 1 or last:
+                nc.sync.dma_start(word_rows[:, cols], y_codes[:, cols].bitcast(I32))
+            elif hi == CHUNKS - 1:
+                shared = slice(CHUNK * first_single, CHUNK * hi)
+                nc.sync.dma_start(word_rows[:, shared], y_codes[:, shared].bitcast(I32))
 
-        deal(w_scales[:], scale_raw[:], 2, PASSES)
-        deal_packed(0)
-        finish_x(0)
-        finish_x(1)
-        deal_packed(1)
+        reorder(w_scales[:], scale_raw[:], 1, PASSES)
+        unread = psum.tile([P, BANK], F32, name="acc", bufs=OUT_BANKS)
+        for repeat in range(WARM_PASSES):
+            nc.tensor.matmul_mx(
+                out=unread[:],
+                lhsT=wg_raw[0][:, 0:P].bitcast(FP8X4),
+                lhsT_scale=w_scales[:].bitcast(U8)[4:P, 0:P],
+                rhs=wg_raw[0][:].bitcast(FP8X4),
+                rhs_scale=w_scales[:].bitcast(U8)[4:P, 0:BANK],
+                start=True,
+                stop=True,
+            )
+        reorder_packed(0)
+        gather(PACK - 1, 0, PART)
+        finish_x(0, picked_flat[:, PACK * J - PART : PACK * J + PART].bitcast(BF16))
+        gather(PACK - 1, PART, J - PART)
+        finish_x(1, x_stage(1))
+        reorder_packed(1)
         hidden(0)
-        quantize_wd(0)
-        quantize_wd(1)
+        for b in range(PASSES):
+            quantize_wd(b)
         hidden(1)
-        finish_x(2)
-        hidden(2)
-        finish_x(3)
-        output(0)
-        hidden(3)
-        hidden(4)
-        output(1)
-        hidden(5)
-        hidden(6)
-        output(2)
-        hidden(7)
-        output(3)
-        output(4)
-        output(5)
+        finish_x(2, x_stage(2))
+        for c in range(2, CHUNKS):
+            hidden(c)
+            if c == 2:
+                gather(PACK - 1, J - PART, J)
+                finish_x(3, x_stage(3))
+            for g, (lo, hi) in enumerate(GROUPS):
+                if lo + LAG == c:
+                    output(g)
+        for g, (lo, hi) in enumerate(GROUPS):
+            if lo + LAG >= CHUNKS:
+                output(g)
 
         for quad in range(4):
             queue = nc.scalar if quad % 2 else nc.sync

@@ -258,7 +258,10 @@ def tile_list_sigm_noneP_kernel(
                 shared = slice(CHUNK * first_single, CHUNK * hi)
                 nc.sync.dma_start(word_rows[:, shared], y_codes[:, shared].bitcast(I32))
 
-        reorder(w_scales[:], scale_raw[:], 1, PASSES)
+        nc.scalar.copy(
+            w_scales[:].bitcast(U32).rearrange("p (b t q e) -> p b t q e", b=PASSES, t=PACK, e=RUN // 4),
+            scale_raw[:].bitcast(U32).rearrange("p (b q t e) -> p b t q e", b=PASSES, t=PACK, e=RUN // 4),
+        )
         unread = psum.tile([P, BANK], F32, name="acc", bufs=OUT_BANKS)
         for repeat in range(WARM_PASSES):
             nc.tensor.matmul_mx(

@@ -25,13 +25,17 @@ BANK = 512
 CHUNK = BANK // PACK
 CHUNKS = J // CHUNK
 PART = 2 * CHUNK
-PARTS = J // PART
-GROUPS = [(0, 2), (2, 4), (4, 5), (5, 6), (6, 7), (7, 8)]
-LAG = 3
-GATE_BUFS = 8
-STAGE_BANKS = 3
+X_PARTS = [(0, 2), (2, 4), (4, 6), (6, 8)]
+GROUPS = [(0, 2), (2, 4), (4, 6), (6, 7), (7, 8)]
+STEPS = CHUNKS * PASSES
+STEP = [(c, b) for lo, hi in [(0, 4), (4, 6), (6, 7), (7, 8)] for b in range(PASSES) for c in range(lo, hi)]
+OUT_TAGS = [("out0", "out1"), ("ga0", "ga1"), ("out0", "out1"), ("ga2",), ("ga0", "ga1")]
+WORD_STORES = [(0, 4), (4, 8)]
+WD_PARTS = [(0, 4), (4, 6), (6, 8)]
+GATE_BYTES = 4 * BANK
+HELD = (7, 14)
+HELD_BYTES = 3 * GATE_BYTES
 WARM_PASSES = 4
-OUT_BANKS = 2
 
 
 def tile_list_sigm_noneP_kernel(
@@ -40,7 +44,7 @@ def tile_list_sigm_noneP_kernel(
     nc = tc.nc
     with ExitStack() as ctx:
         keep = ctx.enter_context(tc.tile_pool(name="keep", bufs=1))
-        ring = ctx.enter_context(tc.tile_pool(name="ring", bufs=GATE_BUFS))
+        laid = ctx.enter_context(tc.tile_pool(name="laid", bufs=1))
         psum = ctx.enter_context(tc.psum_pool(name="psum", bufs=1))
 
         def copy(on_scalar, dst, src):
@@ -104,9 +108,16 @@ def tile_list_sigm_noneP_kernel(
             nc.vector.transpose(weight[:, cols], spread[:, cols])
 
         picked_flat = keep.tile([P, PACK * J + PART], F32, name="picked", align_bytes=64)
+        relay = GATE_BYTES * (STEPS - len(HELD)) + HELD_BYTES * len(HELD)
         picked = picked_flat[:, 0 : PACK * J].rearrange("p (i j) -> p i j", i=PACK)
         x_codes = keep.tile([P, J], U32, name="x_codes", align_bytes=64)
-        x_scales = keep.tile([P, J], U8, name="x_scales", align_bytes=64)
+        def held_at(run):
+            return GATE_BYTES * (STEPS - len(HELD)) + HELD_BYTES * run
+
+        def held(run, name, shape, dtype, first):
+            return laid.tile(shape, dtype, name=name, offset=held_at(run) + first, align_bytes=64)
+
+        x_scales = {}
 
         def gather(i, lo, hi):
             window = x_plane[i][:].indirect(offsets[:, lo // 16 : hi // 16])
@@ -115,19 +126,34 @@ def tile_list_sigm_noneP_kernel(
         for i in range(PACK - 1):
             gather(i, 0, J)
 
-        def finish_x(part, x_bf):
-            cols = slice(PART * part, PART * (part + 1))
-            src = picked[:, :, cols].rearrange("p i (s u) -> p s i u", u=4)
-            dst = x_bf.rearrange("p (s u i) -> p s i u", u=4, i=PACK)
-            copy(part < PARTS - 1, dst, src)
-            quantize(x_codes[:, cols], x_scales[:, cols], x_bf)
+        def weave(engine, words, planes_of):
+            src = planes_of.rearrange("p i (s u) -> p s i u", u=4)
+            dst = words.rearrange("p (s u i) -> p s i u", u=4, i=PACK)
+            if engine is nc.scalar:
+                engine.copy(dst, src)
+            else:
+                engine.tensor_copy(dst, src)
 
-        def x_stage(part):
-            return keep.tile([P, PACK * PART], BF16, name="x_bf%d" % (PART * part), align_bytes=64)[:]
+        def weave_x(part, x_bf):
+            lo, hi = X_PARTS[part]
+            weave(nc.vector if hi == CHUNKS else nc.scalar, x_bf, picked[:, :, CHUNK * lo : CHUNK * hi])
+
+        def quantize_x(part, x_bf):
+            lo, hi = X_PARTS[part]
+            shape = [P, CHUNK * (hi - lo)]
+            x_scales[part] = keep.tile(shape, U8, name="x_scales%d" % part, align_bytes=64)
+            quantize(x_codes[:, CHUNK * lo : CHUNK * hi], x_scales[part][:], x_bf)
+
+        def x_stage(part, name):
+            lo, hi = X_PARTS[part]
+            if part % 2:
+                place = relay + (1536 if part == 1 else 3072)
+                return laid.tile([P, BANK * (hi - lo)], BF16, name=name, offset=place, align_bytes=64)[:]
+            return keep.tile([P, BANK * (hi - lo)], BF16, name=name, align_bytes=64)[:]
 
         w_scales = keep.tile([P, R // 4], I32, name="w_scales", align_bytes=64)
-        wg_codes = [keep.tile([P, PASS_ROWS], I32, name="wg_codes%d" % b, align_bytes=64) for b in range(PASSES)]
-        wu_codes = [keep.tile([P, PASS_ROWS // 2], I32, name="wu_codes%d" % b, align_bytes=64) for b in range(PASSES)]
+        wg_codes = [keep.tile([P, PASS_ROWS], I32, name="wg_codes0", align_bytes=64)]
+        wu_codes = [keep.tile([P, PASS_ROWS // 2], I32, name="wu_codes0", align_bytes=64)]
 
         def reorder(dst, src, column_bytes, passes):
             run = RUN * column_bytes // 4
@@ -136,133 +162,206 @@ def tile_list_sigm_noneP_kernel(
                 src.rearrange("p (b q t e) -> p b t q e", b=passes, t=PACK, e=run),
             )
 
-        def reorder_packed(b):
-            reorder(wg_codes[b][:], wg_raw[b][:], 4, 1)
-            reorder(wu_codes[b][:], wu_raw[b][:], 2, 1)
-
         wd_codes = keep.tile([P, PASSES, N], U32, name="wd_codes", align_bytes=64)
-        wd_scales = keep.tile([P, PASSES, N], U8, name="wd_scales", align_bytes=64)
+        wd_scales = {}
+        wd_bf = {}
 
-        def quantize_wd(b):
-            wd_bf = keep.tile([P, PACK, P, PACK], BF16, name="wd_bf%d" % b, align_bytes=64)
-            for half in range(2):
-                ms = slice(P // 2 * half, P // 2 * (half + 1))
-                src = wd_raw[b][:].rearrange("p t (m i) -> p m t i", i=PACK)[:, ms, :, :]
-                dst = wd_bf[:].rearrange("p i m t -> p m t i")[:, ms, :, :]
-                copy(b == 0 and half == 0, dst, src)
-            quantize(wd_codes[:, b, :], wd_scales[:, b, :], wd_bf[:].rearrange("p i m t -> p (i m t)"))
+        def wd_part(s):
+            return [n for n, (lo, hi) in enumerate(WD_PARTS) if lo <= s < hi][0]
 
-        h_tiles = []
+        def round_wd(lo, hi, engine):
+            part = wd_part(lo)
+            first, end = WD_PARTS[part]
+            if part not in wd_bf:
+                shape = [P, end - first, P, PACK]
+                if part == 0:
+                    wd_bf[part] = laid.tile(shape, BF16, name="wd_bf0", offset=relay + 3072, align_bytes=64)
+                elif engine is nc.vector:
+                    wd_bf[part] = held(0, "wd_bf%d" % part, shape, BF16, 1792)
+                else:
+                    wd_bf[part] = keep.tile(shape, BF16, name="wd_bf%d" % part, align_bytes=64)
+            b, i = divmod(lo, PACK)
+            src = wd_raw[b][:].rearrange("p t (m i) -> p m t i", i=PACK)[:, :, :, i : i + hi - lo]
+            dst = wd_bf[part][:, lo - first : hi - first, :, :].rearrange("p i m t -> p m t i")
+            if engine is nc.scalar:
+                engine.copy(dst, src)
+            else:
+                engine.tensor_copy(dst, src)
+
+        def quantize_wd(part):
+            lo, hi = WD_PARTS[part]
+            shape = [P, P * (hi - lo)]
+            if part == 1:
+                wd_scales[part] = keep.tile(shape, U8, name="wd_scales1", align_bytes=64)
+            else:
+                wd_scales[part] = held(0, "wd_scales%d" % part, shape, U8, 1024 + 256 * part)
+            codes = wd_codes[:].rearrange("p b n -> p (b n)")[:, P * lo : P * hi]
+            quantize(codes, wd_scales[part][:], wd_bf[part][:].rearrange("p i m t -> p (i m t)"))
+
+        def wd_scale(s):
+            first = P * (s - WD_PARTS[wd_part(s)][0])
+            return wd_scales[wd_part(s)][:, first : first + P]
+
+        h_codes, h_scales, h_bf = [], {}, []
         for lo, hi in GROUPS:
             width = CHUNK * (hi - lo)
-            codes = keep.tile([P, PASSES, width], U32, name="h_codes%d" % lo, align_bytes=64)
-            scales = keep.tile([P, PASSES, width], U8, name="h_scales%d" % lo, align_bytes=64)
-            h_bf = keep.tile([P, PASSES, width, PACK], BF16, name="h_bf%d" % lo, align_bytes=64)
-            h_tiles.append((codes, scales, h_bf))
+            h_codes.append(keep.tile([P, PASSES, width], U32, name="h_codes%d" % lo, align_bytes=64))
+            h_bf.append(keep.tile([P, PASSES, width, PACK], BF16, name="words%d" % lo, align_bytes=64))
+        gates = {}
 
-        def hidden(c):
-            cols = slice(CHUNK * c, CHUNK * (c + 1))
-            g = [g for g, (lo, hi) in enumerate(GROUPS) if lo <= c < hi][0]
-            lo, hi = GROUPS[g]
-            codes, scales, h_bf = h_tiles[g]
-            inner = slice(CHUNK * (c - lo), CHUNK * (c - lo + 1))
-            last = c == CHUNKS - 1
-            for b in range(PASSES):
-                ga = psum.tile([P, PACK, CHUNK], F32, name="ga", bufs=STAGE_BANKS)
-                ub = psum.tile([P, PACK, CHUNK], F32, name="ub", bufs=STAGE_BANKS)
-                for t in range(PACK):
-                    first = b * PASS_ROWS + t * P
-                    nc.tensor.matmul_mx(
-                        out=ga[:, t, :],
-                        lhsT=wg_codes[b][:, t * P : (t + 1) * P].bitcast(FP8X4),
-                        lhsT_scale=w_scales[:].bitcast(U8)[4:P, first : first + P],
-                        rhs=x_codes[:, cols].bitcast(FP8X4),
-                        rhs_scale=x_scales[:, cols],
-                        start=True,
-                        stop=True,
-                    )
-                for t in range(PACK):
-                    first = b * PASS_ROWS + t * P
-                    nc.tensor.matmul_mx(
-                        out=ub[:, t, :],
-                        lhsT=wu_codes[b][:].bitcast(U8)[:, 2 * t * P : 2 * (t + 1) * P].bitcast(FP4X4),
-                        lhsT_scale=w_scales[:].bitcast(U8)[:, first : first + P],
-                        rhs=x_codes[:, cols].bitcast(FP8X4),
-                        rhs_scale=x_scales[:, cols],
-                        start=True,
-                        stop=True,
-                    )
-                gate = ring.tile([P, CHUNK, PACK], F32, name="gate")
-                nc.scalar.activation(gate[:], ga[:].rearrange("p t j -> p j t"), SIGMOID)
-                nc.vector.tensor_tensor(h_bf[:, b, inner, :], ub[:].rearrange("p t j -> p j t"), gate[:], MULT)
-                if last:
-                    quantize(codes[:, b, :], scales[:, b, :], h_bf[:, b, :, :].rearrange("p j t -> p (j t)"))
-            if hi == c + 1 and not last:
-                quantize(
-                    codes[:].rearrange("p b j -> p (b j)"),
-                    scales[:].rearrange("p b j -> p (b j)"),
-                    h_bf[:].rearrange("p b j t -> p (b j t)"),
+        def bank(tag, slices, width):
+            return psum.tile([P, slices, width], F32, name=tag, bufs=1)
+
+        def first_product(step, acc, codes, column_bytes, dtype, scale_row):
+            c, b = STEP[step]
+            part = [n for n, (lo, hi) in enumerate(X_PARTS) if lo <= c < hi][0]
+            inner = slice(CHUNK * (c - X_PARTS[part][0]), CHUNK * (c - X_PARTS[part][0] + 1))
+            for t in range(PACK):
+                first = b * PASS_ROWS + t * P
+                nc.tensor.matmul_mx(
+                    out=acc[:, t, :],
+                    lhsT=codes[b][:].bitcast(U8)[:, column_bytes * t * P : column_bytes * (t + 1) * P].bitcast(dtype),
+                    lhsT_scale=w_scales[:].bitcast(U8)[scale_row:P, first : first + P],
+                    rhs=x_codes[:, CHUNK * c : CHUNK * (c + 1)].bitcast(FP8X4),
+                    rhs_scale=x_scales[part][:, inner],
+                    start=True,
+                    stop=True,
                 )
 
-        y_codes = keep.tile([P, J], U32, name="y_codes", align_bytes=64)
-        y_scales = keep.tile([P, J], U8, name="y_scales", align_bytes=64)
+        def gate(step):
+            ga = bank(("ga0", "ga1", "ga2", "ga2")[step - 12] if step >= 12 else "ga%d" % (step % 3), PACK, CHUNK)
+            first_product(step, ga, wg_codes, 4, FP8X4, 4)
+            if step in HELD:
+                place = held_at(HELD.index(step))
+            else:
+                place = GATE_BYTES * (step - len([other for other in HELD if other < step]))
+            gates[step] = laid.tile([P, CHUNK, PACK], F32, name="gate%d" % step, offset=place, align_bytes=64)
+            nc.scalar.activation(gates[step][:], ga[:].rearrange("p t j -> p j t"), SIGMOID)
+
+        def group_of(c):
+            return [g for g, (lo, hi) in enumerate(GROUPS) if lo <= c < hi][0]
+
+        ups = {}
+
+        def up(step):
+            tags = ["ub0", "ub1", "ub2", "out0", "out1"]
+            ups[step] = bank(tags[step % 5] if step < 9 else tags[step % 3], PACK, CHUNK)
+            first_product(step, ups[step], wu_codes, 2, FP4X4, 0)
+
+        def multiply(step):
+            c, b = STEP[step]
+            g = group_of(c)
+            inner = slice(CHUNK * (c - GROUPS[g][0]), CHUNK * (c - GROUPS[g][0] + 1))
+            ub = ups[step][:].rearrange("p t j -> p j t")
+            nc.vector.tensor_tensor(h_bf[g][:, b, inner, :], ub, gates[step][:], MULT)
+
+        def quantize_h(g, passes):
+            width = CHUNK * (GROUPS[g][1] - GROUPS[g][0])
+            if g not in h_scales:
+                if g == 0:
+                    h_scales[g] = held(0, "h_scales0", [P, PASSES, width], U8, 512)
+                elif g == 1:
+                    h_scales[g] = held(0, "h_scales1", [P, PASSES, width], U8, 0)
+                elif g == 3:
+                    h_scales[g] = held(1, "h_scales3", [P, PASSES, width], U8, 0)
+                else:
+                    h_scales[g] = keep.tile([P, PASSES, width], U8, name="h_scales%d" % g, align_bytes=64)
+            quantize(
+                h_codes[g][:, passes, :].rearrange("p b j -> p (b j)"),
+                h_scales[g][:, passes, :].rearrange("p b j -> p (b j)"),
+                h_bf[g][:, passes, :, :].rearrange("p b j t -> p (b j t)"),
+            )
+
+        y_scales = keep.tile([P, PART], U8, name="y_scales", align_bytes=64)
         y_rows = out_0.rearrange("(p i) j -> p i j", i=PACK)
         word_rows = out_1[0].rearrange("p j i -> p (j i)").bitcast(I32)
-        first_single = [lo for lo, hi in GROUPS if hi - lo == 1][0]
+
+        y_tiles = {}
 
         def output(g):
             lo, hi = GROUPS[g]
             width = CHUNK * (hi - lo)
-            cols = slice(CHUNK * lo, CHUNK * hi)
             last = hi == CHUNKS
-            codes, scales, h_bf = h_tiles[g]
+            source = group_of(lo)
+            inner = slice(CHUNK * (lo - GROUPS[source][0]), CHUNK * (hi - GROUPS[source][0]))
             y = keep.tile([P, PACK, width], F32, name="y%d" % lo)
-            y_bf = keep.tile([P, width, PACK], BF16, name="y_bf%d" % lo, align_bytes=64)
+            y_tiles[g] = y
             per_bank = PACK // 2 if last else BANK // width
-            tag, bufs = ("ga", STAGE_BANKS) if last else ("acc", OUT_BANKS)
-            banks = [psum.tile([P, per_bank, width], F32, name=tag, bufs=bufs) for slot in range(PACK // per_bank)]
+            slots = range(PACK // per_bank)
+            banks = [bank(OUT_TAGS[g][slot], per_bank, width) for slot in slots]
 
             def product(i, b, start, stop):
                 nc.tensor.matmul_mx(
                     out=banks[i // per_bank][:, i % per_bank, :],
                     lhsT=wd_codes[:, b, P * i : P * (i + 1)].bitcast(FP8X4),
-                    lhsT_scale=wd_scales[:, b, P * i : P * (i + 1)],
-                    rhs=codes[:, b, :].bitcast(FP8X4),
-                    rhs_scale=scales[:, b, :],
+                    lhsT_scale=wd_scale(PACK * b + i),
+                    rhs=h_codes[source][:, b, inner].bitcast(FP8X4),
+                    rhs_scale=h_scales[source][:, b, inner],
                     start=start,
                     stop=stop,
                 )
 
-            if last:
+            if g == 0:
                 for b in range(PASSES):
                     for i in range(PACK):
                         product(i, b, b == 0 and i % per_bank == 0, b == PASSES - 1 and i % per_bank == per_bank - 1)
-                for slot, bank in enumerate(banks):
-                    copy(slot == 0, y[:, slot * per_bank : (slot + 1) * per_bank, :], bank[:])
+                for slot, acc in enumerate(banks):
+                    part = slice(slot * per_bank, (slot + 1) * per_bank)
+                    nc.scalar.copy(y[:, part, :], acc[:])
+                    nc.sync.dma_start(y_rows[:, part, CHUNK * lo : CHUNK * hi], y[:, part, :])
             else:
-                for slot, bank in enumerate(banks):
+                for slot, acc in enumerate(banks):
                     for i in range(slot * per_bank, (slot + 1) * per_bank):
                         for b in range(PASSES):
                             product(i, b, b == 0, b == PASSES - 1)
-                    nc.scalar.copy(y[:, slot * per_bank : (slot + 1) * per_bank, :], bank[:])
-            nc.sync.dma_start(y_rows[:, :, cols], y[:])
-            copy(
-                hi - lo > 1,
-                y_bf[:].rearrange("p (s u) i -> p s i u", u=4),
-                y[:].rearrange("p i (s u) -> p s i u", u=4),
-            )
-            quantize(y_codes[:, cols], y_scales[:, cols], y_bf[:].rearrange("p j i -> p (j i)"))
-            if hi - lo > 1 or last:
-                nc.sync.dma_start(word_rows[:, cols], y_codes[:, cols].bitcast(I32))
-            elif hi == CHUNKS - 1:
-                shared = slice(CHUNK * first_single, CHUNK * hi)
-                nc.sync.dma_start(word_rows[:, shared], y_codes[:, shared].bitcast(I32))
+                    part = slice(slot * per_bank, (slot + 1) * per_bank)
+                    copy(not last or slot == 1, y[:, part, :], acc[:])
+                    if not last:
+                        nc.sync.dma_start(y_rows[:, part, CHUNK * lo : CHUNK * hi], y[:, part, :])
+            if last:
+                nc.sync.dma_start(y_rows[:, :, CHUNK * lo : CHUNK * hi], y[:])
+
+        y_bf = {}
+
+        def weave_y(g, engine, picks=None):
+            lo, hi = GROUPS[g]
+            shape = [P, BANK * (hi - lo)]
+            if g in y_bf:
+                pass
+            elif engine is nc.gpsimd:
+                y_bf[g] = keep.tile(shape, BF16, name="words4", align_bytes=64)
+            elif g == 2:
+                y_bf[g] = keep.tile(shape, BF16, name="words6", align_bytes=64)
+            else:
+                y_bf[g] = keep.tile(shape, BF16, name="y_bf%d" % lo, align_bytes=64)
+            if picks:
+                weave(engine, y_bf[g][:, PACK * picks.start : PACK * picks.stop], y_tiles[g][:, :, picks])
+            else:
+                weave(engine, y_bf[g][:], y_tiles[g][:])
+
+        y_codes, done = {}, []
+
+        def planes(g):
+            lo, hi = GROUPS[g]
+            first, end = [(a, z) for a, z in WORD_STORES if a <= lo < z][0]
+            if first not in y_codes:
+                shape = [P, CHUNK * (end - first)]
+                if first < 4:
+                    y_codes[first] = held(1, "y_codes%d" % first, shape, U32, 256)
+                else:
+                    y_codes[first] = keep.tile(shape, U32, name="y_codes%d" % first, align_bytes=64)
+            codes = y_codes[first][:, CHUNK * (lo - first) : CHUNK * (hi - first)]
+            pair, first_col = divmod(CHUNK * lo, PART)
+            quantize(codes, y_scales[4 * pair : P, first_col : first_col + CHUNK * (hi - lo)], y_bf[g][:])
+            done.append(g)
+            if all(n in done for n, (a, e) in enumerate(GROUPS) if first <= a < end):
+                nc.sync.dma_start(word_rows[:, CHUNK * first : CHUNK * end], y_codes[first][:].bitcast(I32))
 
         nc.scalar.copy(
             w_scales[:].bitcast(U32).rearrange("p (b t q e) -> p b t q e", b=PASSES, t=PACK, e=RUN // 4),
             scale_raw[:].bitcast(U32).rearrange("p (b q t e) -> p b t q e", b=PASSES, t=PACK, e=RUN // 4),
         )
-        unread = psum.tile([P, BANK], F32, name="acc", bufs=OUT_BANKS)
+        unread = psum.tile([P, BANK], F32, name="ub2", bufs=1)
         for repeat in range(WARM_PASSES):
             nc.tensor.matmul_mx(
                 out=unread[:],
@@ -273,32 +372,80 @@ def tile_list_sigm_noneP_kernel(
                 start=True,
                 stop=True,
             )
-        reorder_packed(0)
+        both = slice(0, PASSES)
+        x_bf = [picked_flat[:, PACK * J - PART : PACK * J + PART].bitcast(BF16)]
+        x_bf.extend(x_stage(part, name) for part, name in ((1, "x_bf1"), (2, "x_bf2")))
         gather(PACK - 1, 0, PART)
-        finish_x(0, picked_flat[:, PACK * J - PART : PACK * J + PART].bitcast(BF16))
         gather(PACK - 1, PART, J - PART)
-        finish_x(1, x_stage(1))
-        reorder_packed(1)
-        hidden(0)
+        for part in range(3):
+            weave_x(part, x_bf[part])
+        quantize_x(0, x_bf[0])
+        reorder(wg_codes[0][:], wg_raw[0][:], 4, 1)
+        reorder(wu_codes[0][:], wu_raw[0][:], 2, 1)
+        gather(PACK - 1, J - PART, J)
+        quantize_x(1, x_bf[1])
+        wg_codes.append(laid.tile([P, PASS_ROWS], I32, name="wg_codes1", offset=relay, align_bytes=64))
+        wu_codes.append(laid.tile([P, PASS_ROWS // 2], I32, name="wu_codes1", offset=relay + 2048, align_bytes=64))
+        x_bf.append(x_stage(3, "x_bf3"))
+        reorder(wg_codes[1][:], wg_raw[1][:], 4, 1)
+        weave_x(3, x_bf[3])
+        reorder(wu_codes[1][:], wu_raw[1][:], 2, 1)
+        quantize_x(2, x_bf[2])
+        quantize_x(3, x_bf[3])
+        round_wd(0, 4, nc.gpsimd)
+        for step in range(3):
+            gate(step)
+        for step in range(9):
+            up(step)
+            multiply(step)
+            if step == 6:
+                round_wd(6, 8, nc.scalar)
+            gate(step + 3)
+        round_wd(4, 6, nc.vector)
+        quantize_wd(0)
+        quantize_h(0, both)
+        quantize_wd(2)
+        quantize_wd(1)
+        quantize_h(1, both)
+        up(9)
+        multiply(9)
+        gate(12)
+        gate(13)
+        up(10)
+        output(0)
+        gate(14)
+        gate(15)
+        multiply(10)
+        up(11)
+        multiply(11)
+        up(12)
+        output(1)
         for b in range(PASSES):
-            quantize_wd(b)
-        hidden(1)
-        finish_x(2, x_stage(2))
-        for c in range(2, CHUNKS):
-            hidden(c)
-            if c == 2:
-                gather(PACK - 1, J - PART, J)
-                finish_x(3, x_stage(3))
-            for g, (lo, hi) in enumerate(GROUPS):
-                if lo + LAG == c:
-                    output(g)
-        for g, (lo, hi) in enumerate(GROUPS):
-            if lo + LAG >= CHUNKS:
-                output(g)
+            quantize_h(2, slice(b, b + 1))
+        weave_y(0, nc.gpsimd)
+        multiply(12)
+        for step in range(13, 16):
+            up(step)
+            multiply(step)
+        weave_y(1, nc.scalar, slice(0, CHUNK))
+        output(2)
+        weave_y(1, nc.scalar, slice(CHUNK, PART))
+        quantize_h(3, both)
+        quantize_h(4, both)
+        output(3)
+        output(4)
+        planes(0)
+        weave_y(2, nc.vector)
+        planes(1)
+        planes(2)
+        weave_y(3, nc.scalar)
+        weave_y(4, nc.vector)
+        planes(3)
+        planes(4)
 
         for quad in range(4):
             queue = nc.scalar if quad % 2 else nc.sync
             queue.dma_start(
-                out_2[0, 4 * quad : 4 * quad + 4, :].bitcast(I32),
-                y_scales[32 * quad : 32 * quad + 4, :].bitcast(I32),
+                out_2[0, 4 * quad : 4 * quad + 4, :].bitcast(I32).rearrange("r (c u) -> c r u", c=4),
+                y_scales[32 * quad : 32 * quad + 16, :].bitcast(I32),
             )

@@ -127,8 +127,9 @@ def tile_list_sigm_noneP_kernel(
             gather(i, 0, J)
 
         def weave(engine, words, planes_of):
-            src = planes_of.rearrange("p i (s u) -> p s i u", u=4)
-            dst = words.rearrange("p (s u i) -> p s i u", u=4, i=PACK)
+            u = 2 if engine is nc.scalar else 4
+            src = planes_of.rearrange("p i (s u) -> p s i u", u=u)
+            dst = words.rearrange("p (s u i) -> p s i u", u=u, i=PACK)
             if engine is nc.scalar:
                 engine.copy(dst, src)
             else:

@@ -25,17 +25,17 @@ BANK = 512
 CHUNK = BANK // PACK
 CHUNKS = J // CHUNK
 PART = 2 * CHUNK
-X_PARTS = [(0, 2), (2, 4), (4, 6), (6, 8)]
+X_PARTS = [(0, 1), (1, 2), (2, 4), (4, 6), (6, 8)]
 GROUPS = [(0, 2), (2, 4), (4, 6), (6, 7), (7, 8)]
 STEPS = CHUNKS * PASSES
-STEP = [(c, b) for lo, hi in [(0, 4), (4, 6), (6, 7), (7, 8)] for b in range(PASSES) for c in range(lo, hi)]
-OUT_TAGS = [("out0", "out1"), ("ga0", "ga1"), ("out0", "out1"), ("ga2",), ("ga0", "ga1")]
-WORD_STORES = [(0, 4), (4, 8)]
+STEP = [(c, b) for lo, hi in GROUPS for b in range(PASSES) for c in range(lo, hi)]
+OUT_TAGS = [("out0", "out1"), ("ga1", "ga2"), ("out1", "out0"), ("ga0",), ("ga1", "ga2")]
+WORD_STORES = [(0, 2), (2, 6), (6, 8)]
 WD_PARTS = [(0, 4), (4, 6), (6, 8)]
 GATE_BYTES = 4 * BANK
-HELD = (7, 14)
+HELD = (8, 14)
 HELD_BYTES = 3 * GATE_BYTES
-WARM_PASSES = 4
+WARM_PASSES = 8
 
 
 def tile_list_sigm_noneP_kernel(
@@ -66,11 +66,14 @@ def tile_list_sigm_noneP_kernel(
                 nc.sync.dma_start(scale_raw[rows, :], source[0, 4 * quad : 4 * quad + 4, :].bitcast(I32))
 
         x_rows = xT.rearrange("(p i) t -> i p t", i=PACK)
+        relay = GATE_BYTES * (STEPS - len(HELD)) + HELD_BYTES * len(HELD)
         x_plane = [keep.tile([P, T], F32, name="x_plane%d" % i) for i in range(PACK)]
         weight = keep.tile([P, J], F32, name="weight", align_bytes=64)
         w_piece = keep.tile([P, J // 16], F32, name="w_piece", align_bytes=64)
-        wg_raw = [keep.tile([P, PASS_ROWS], I32, name="wg_raw%d" % b, align_bytes=64) for b in range(PASSES)]
-        wu_raw = [keep.tile([P, PASS_ROWS // 2], I32, name="wu_raw%d" % b) for b in range(PASSES)]
+        wg_raw = [keep.tile([P, PASS_ROWS], I32, name="wg_raw0", align_bytes=64)]
+        wu_raw = [keep.tile([P, PASS_ROWS // 2], I32, name="wu_raw0")]
+        wg_raw.append(laid.tile([P, PASS_ROWS], I32, name="wg_raw1", offset=relay, align_bytes=64))
+        wu_raw.append(laid.tile([P, PASS_ROWS // 2], I32, name="wu_raw1", offset=relay + 2048, align_bytes=64))
         wd_raw = [keep.tile([P, PACK, N], F32, name="wd_raw%d" % b) for b in range(PASSES)]
         wg_hbm = wg_words[0].rearrange("p r i -> p (r i)").bitcast(I32)
         wu_hbm = wu_words[0].bitcast(I32)
@@ -82,14 +85,23 @@ def tile_list_sigm_noneP_kernel(
         load_scales(wu_scales, 0)
         nc.sync.dma_start(x_plane[2][:], x_rows[2])
         load_scales(wg_scales, 4)
+        half = PASS_ROWS // 2
         nc.sync.dma_start(x_plane[3][:], x_rows[3])
-        for b in range(PASSES):
+        nc.sync.dma_start(wg_raw[0][:, 0:half], wg_hbm[:, 0:half])
+        nc.sync.dma_start(wg_raw[0][:, half:PASS_ROWS], wg_hbm[:, half:PASS_ROWS])
+        nc.sync.dma_start(wu_raw[0][:], wu_hbm[:, 0:half])
+
+        def load_packed(b):
             nc.sync.dma_start(wg_raw[b][:], wg_hbm[:, PASS_ROWS * b : PASS_ROWS * (b + 1)])
             nc.sync.dma_start(wu_raw[b][:], wu_hbm[:, PASS_ROWS // 2 * b : PASS_ROWS // 2 * (b + 1)])
-        for b in range(PASSES):
+
+        def load_wd(b, t):
             rows = wd[PASS_ROWS * b : PASS_ROWS * (b + 1), :].rearrange("(q t e) n -> t q e n", t=PACK, e=RUN)
-            for t in range(PACK):
-                nc.sync.dma_start(wd_raw[b][:, t, :], rows[t])
+            nc.sync.dma_start(wd_raw[b][:, t, :], rows[t])
+
+        load_packed(1)
+        for s in range(PASSES * PACK):
+            load_wd(s // PACK, s % PACK)
 
         warm = keep.tile([P, 1], F32, name="warm")
         warm_out = keep.tile([P, 1], F32, name="warm_out")
@@ -107,9 +119,8 @@ def tile_list_sigm_noneP_kernel(
             copy(half == 1, dst, src.unsqueeze(3).broadcast_to([P, 8, 4, 16]))
             nc.vector.transpose(weight[:, cols], spread[:, cols])
 
-        picked_flat = keep.tile([P, PACK * J + PART], F32, name="picked", align_bytes=64)
-        relay = GATE_BYTES * (STEPS - len(HELD)) + HELD_BYTES * len(HELD)
-        picked = picked_flat[:, 0 : PACK * J].rearrange("p (i j) -> p i j", i=PACK)
+        picked_flat = keep.tile([P, PACK * J], F32, name="picked", align_bytes=64)
+        picked = picked_flat[:].rearrange("p (i j) -> p i j", i=PACK)
         x_codes = keep.tile([P, J], U32, name="x_codes", align_bytes=64)
         def held_at(run):
             return GATE_BYTES * (STEPS - len(HELD)) + HELD_BYTES * run
@@ -137,28 +148,32 @@ def tile_list_sigm_noneP_kernel(
 
         def weave_x(part, x_bf):
             lo, hi = X_PARTS[part]
-            weave(nc.vector if hi == CHUNKS else nc.scalar, x_bf, picked[:, :, CHUNK * lo : CHUNK * hi])
+            engine = [nc.scalar, nc.scalar, nc.scalar, nc.vector, nc.gpsimd][part]
+            weave(engine, x_bf, picked[:, :, CHUNK * lo : CHUNK * hi])
 
         def quantize_x(part, x_bf):
             lo, hi = X_PARTS[part]
             shape = [P, CHUNK * (hi - lo)]
-            x_scales[part] = keep.tile(shape, U8, name="x_scales%d" % part, align_bytes=64)
+            if part == 4:
+                x_scales[part] = held(0, "x_scales4", shape, U8, 0)
+            else:
+                x_scales[part] = keep.tile(shape, U8, name="x_scales%d" % part, align_bytes=64)
             quantize(x_codes[:, CHUNK * lo : CHUNK * hi], x_scales[part][:], x_bf)
 
         def x_stage(part, name):
             lo, hi = X_PARTS[part]
-            if part % 2:
-                place = relay + (1536 if part == 1 else 3072)
-                return laid.tile([P, BANK * (hi - lo)], BF16, name=name, offset=place, align_bytes=64)[:]
-            return keep.tile([P, BANK * (hi - lo)], BF16, name=name, align_bytes=64)[:]
+            place = relay + {1: 3072, 2: 4096, 3: 1984, 4: 4096}[part]
+            return laid.tile([P, BANK * (hi - lo)], BF16, name=name, offset=place, align_bytes=64)[:]
 
         w_scales = keep.tile([P, R // 4], I32, name="w_scales", align_bytes=64)
         wg_codes = [keep.tile([P, PASS_ROWS], I32, name="wg_codes0", align_bytes=64)]
         wu_codes = [keep.tile([P, PASS_ROWS // 2], I32, name="wu_codes0", align_bytes=64)]
 
-        def reorder(dst, src, column_bytes, passes):
+        def reorder(dst, src, column_bytes, passes, on_scalar=False):
             run = RUN * column_bytes // 4
-            nc.vector.tensor_copy(
+            dst, src = dst.bitcast(U32), src.bitcast(U32)
+            copy(
+                on_scalar,
                 dst.rearrange("p (b t q e) -> p b t q e", b=passes, t=PACK, e=run),
                 src.rearrange("p (b q t e) -> p b t q e", b=passes, t=PACK, e=run),
             )
@@ -170,20 +185,16 @@ def tile_list_sigm_noneP_kernel(
         def wd_part(s):
             return [n for n, (lo, hi) in enumerate(WD_PARTS) if lo <= s < hi][0]
 
-        def round_wd(lo, hi, engine):
+        def round_wd(lo, hi, engine, columns=slice(0, P)):
             part = wd_part(lo)
             first, end = WD_PARTS[part]
             if part not in wd_bf:
                 shape = [P, end - first, P, PACK]
-                if part == 0:
-                    wd_bf[part] = laid.tile(shape, BF16, name="wd_bf0", offset=relay + 3072, align_bytes=64)
-                elif engine is nc.vector:
-                    wd_bf[part] = held(0, "wd_bf%d" % part, shape, BF16, 1792)
-                else:
-                    wd_bf[part] = keep.tile(shape, BF16, name="wd_bf%d" % part, align_bytes=64)
+                place = GATE_BYTES * (0, 2, 7)[part]
+                wd_bf[part] = laid.tile(shape, BF16, name="wd_bf%d" % part, offset=place, align_bytes=64)
             b, i = divmod(lo, PACK)
-            src = wd_raw[b][:].rearrange("p t (m i) -> p m t i", i=PACK)[:, :, :, i : i + hi - lo]
-            dst = wd_bf[part][:, lo - first : hi - first, :, :].rearrange("p i m t -> p m t i")
+            src = wd_raw[b][:].rearrange("p t (m i) -> p m t i", i=PACK)[:, columns, :, i : i + hi - lo]
+            dst = wd_bf[part][:, lo - first : hi - first, columns, :].rearrange("p i m t -> p m t i")
             if engine is nc.scalar:
                 engine.copy(dst, src)
             else:
@@ -192,10 +203,7 @@ def tile_list_sigm_noneP_kernel(
         def quantize_wd(part):
             lo, hi = WD_PARTS[part]
             shape = [P, P * (hi - lo)]
-            if part == 1:
-                wd_scales[part] = keep.tile(shape, U8, name="wd_scales1", align_bytes=64)
-            else:
-                wd_scales[part] = held(0, "wd_scales%d" % part, shape, U8, 1024 + 256 * part)
+            wd_scales[part] = held(0, "wd_scales%d" % part, shape, U8, (768, 1280, 1536)[part])
             codes = wd_codes[:].rearrange("p b n -> p (b n)")[:, P * lo : P * hi]
             quantize(codes, wd_scales[part][:], wd_bf[part][:].rearrange("p i m t -> p (i m t)"))
 
@@ -230,7 +238,7 @@ def tile_list_sigm_noneP_kernel(
                 )
 
         def gate(step):
-            ga = bank(("ga0", "ga1", "ga2", "ga2")[step - 12] if step >= 12 else "ga%d" % (step % 3), PACK, CHUNK)
+            ga = bank("out0" if step == STEPS - 1 else "ga%d" % (step % 3), PACK, CHUNK)
             first_product(step, ga, wg_codes, 4, FP8X4, 4)
             if step in HELD:
                 place = held_at(HELD.index(step))
@@ -246,7 +254,7 @@ def tile_list_sigm_noneP_kernel(
 
         def up(step):
             tags = ["ub0", "ub1", "ub2", "out0", "out1"]
-            ups[step] = bank(tags[step % 5] if step < 9 else tags[step % 3], PACK, CHUNK)
+            ups[step] = bank(tags[step % 5] if step < 10 else ("ub1", "ub2", "ub0", "ga0", "ub1", "ub2")[step - 10], PACK, CHUNK)
             first_product(step, ups[step], wu_codes, 2, FP4X4, 0)
 
         def multiply(step):
@@ -260,9 +268,9 @@ def tile_list_sigm_noneP_kernel(
             width = CHUNK * (GROUPS[g][1] - GROUPS[g][0])
             if g not in h_scales:
                 if g == 0:
-                    h_scales[g] = held(0, "h_scales0", [P, PASSES, width], U8, 512)
+                    h_scales[g] = held(0, "h_scales0", [P, PASSES, width], U8, 256)
                 elif g == 1:
-                    h_scales[g] = held(0, "h_scales1", [P, PASSES, width], U8, 0)
+                    h_scales[g] = held(0, "h_scales1", [P, PASSES, width], U8, 1792)
                 elif g == 3:
                     h_scales[g] = held(1, "h_scales3", [P, PASSES, width], U8, 0)
                 else:
@@ -273,23 +281,32 @@ def tile_list_sigm_noneP_kernel(
                 h_bf[g][:, passes, :, :].rearrange("p b j t -> p (b j t)"),
             )
 
-        y_scales = keep.tile([P, PART], U8, name="y_scales", align_bytes=64)
+        y_scales = keep.tile([P, J // 2], U8, name="y_scales", align_bytes=64)
         y_rows = out_0.rearrange("(p i) j -> p i j", i=PACK)
         word_rows = out_1[0].rearrange("p j i -> p (j i)").bitcast(I32)
 
-        y_tiles = {}
+        y_tiles, y_banks = {}, {}
 
-        def output(g):
+        def output(g, only=None):
             lo, hi = GROUPS[g]
             width = CHUNK * (hi - lo)
             last = hi == CHUNKS
             source = group_of(lo)
             inner = slice(CHUNK * (lo - GROUPS[source][0]), CHUNK * (hi - GROUPS[source][0]))
-            y = keep.tile([P, PACK, width], F32, name="y%d" % lo)
-            y_tiles[g] = y
+            if g in y_tiles:
+                pass
+            elif width == PART:
+                y_tiles[g] = keep.tile([P, PACK, PART], F32, name="y%d" % lo)[:]
+            else:
+                if not last:
+                    y_tiles["pair"] = keep.tile([P, PACK, PART], F32, name="y%d" % lo)
+                y_tiles[g] = y_tiles["pair"][:, :, CHUNK * (lo % 2) : CHUNK * (lo % 2 + 1)]
             per_bank = PACK // 2 if last else BANK // width
             slots = range(PACK // per_bank)
-            banks = [bank(OUT_TAGS[g][slot], per_bank, width) for slot in slots]
+            banks = y_banks.setdefault(g, {})
+            slots = slots if only is None else [only]
+            for slot in slots:
+                banks[slot] = bank(OUT_TAGS[g][slot], per_bank, width)
 
             def product(i, b, start, stop):
                 nc.tensor.matmul_mx(
@@ -306,21 +323,21 @@ def tile_list_sigm_noneP_kernel(
                 for b in range(PASSES):
                     for i in range(PACK):
                         product(i, b, b == 0 and i % per_bank == 0, b == PASSES - 1 and i % per_bank == per_bank - 1)
-                for slot, acc in enumerate(banks):
-                    part = slice(slot * per_bank, (slot + 1) * per_bank)
-                    nc.scalar.copy(y[:, part, :], acc[:])
-                    nc.sync.dma_start(y_rows[:, part, CHUNK * lo : CHUNK * hi], y[:, part, :])
             else:
-                for slot, acc in enumerate(banks):
+                for slot in slots:
                     for i in range(slot * per_bank, (slot + 1) * per_bank):
                         for b in range(PASSES):
                             product(i, b, b == 0, b == PASSES - 1)
-                    part = slice(slot * per_bank, (slot + 1) * per_bank)
-                    copy(not last or slot == 1, y[:, part, :], acc[:])
-                    if not last:
-                        nc.sync.dma_start(y_rows[:, part, CHUNK * lo : CHUNK * hi], y[:, part, :])
-            if last:
-                nc.sync.dma_start(y_rows[:, :, CHUNK * lo : CHUNK * hi], y[:])
+
+        def leave(g, slot, on_scalar=True):
+            lo, hi = GROUPS[g]
+            y, per_bank = y_tiles[g], PACK // len(OUT_TAGS[g])
+            part = slice(slot * per_bank, (slot + 1) * per_bank)
+            copy(on_scalar, y[:, part, :], y_banks[g][slot][:])
+            if hi - lo == 2:
+                nc.sync.dma_start(y_rows[:, part, CHUNK * lo : CHUNK * hi], y[:, part, :])
+            elif hi == CHUNKS:
+                nc.sync.dma_start(y_rows[:, part, J - PART : J], y_tiles["pair"][:, part, :])
 
         y_bf = {}
 
@@ -331,14 +348,14 @@ def tile_list_sigm_noneP_kernel(
                 pass
             elif engine is nc.gpsimd:
                 y_bf[g] = keep.tile(shape, BF16, name="words4", align_bytes=64)
-            elif g == 2:
-                y_bf[g] = keep.tile(shape, BF16, name="words6", align_bytes=64)
+            elif g < 3:
+                y_bf[g] = keep.tile(shape, BF16, name="words%d" % (5 + g), align_bytes=64)
             else:
                 y_bf[g] = keep.tile(shape, BF16, name="y_bf%d" % lo, align_bytes=64)
             if picks:
                 weave(engine, y_bf[g][:, PACK * picks.start : PACK * picks.stop], y_tiles[g][:, :, picks])
             else:
-                weave(engine, y_bf[g][:], y_tiles[g][:])
+                weave(engine, y_bf[g][:], y_tiles[g])
 
         y_codes, done = {}, []
 
@@ -347,12 +364,12 @@ def tile_list_sigm_noneP_kernel(
             first, end = [(a, z) for a, z in WORD_STORES if a <= lo < z][0]
             if first not in y_codes:
                 shape = [P, CHUNK * (end - first)]
-                if first < 4:
-                    y_codes[first] = held(1, "y_codes%d" % first, shape, U32, 256)
+                if first == 0:
+                    y_codes[first] = held(1, "y_codes%d" % first, shape, U32, 256 + 512 * first)
                 else:
                     y_codes[first] = keep.tile(shape, U32, name="y_codes%d" % first, align_bytes=64)
             codes = y_codes[first][:, CHUNK * (lo - first) : CHUNK * (hi - first)]
-            pair, first_col = divmod(CHUNK * lo, PART)
+            pair, first_col = divmod(CHUNK * lo, J // 2)
             quantize(codes, y_scales[4 * pair : P, first_col : first_col + CHUNK * (hi - lo)], y_bf[g][:])
             done.append(g)
             if all(n in done for n, (a, e) in enumerate(GROUPS) if first <= a < end):
@@ -362,84 +379,105 @@ def tile_list_sigm_noneP_kernel(
             w_scales[:].bitcast(U32).rearrange("p (b t q e) -> p b t q e", b=PASSES, t=PACK, e=RUN // 4),
             scale_raw[:].bitcast(U32).rearrange("p (b q t e) -> p b t q e", b=PASSES, t=PACK, e=RUN // 4),
         )
-        unread = psum.tile([P, BANK], F32, name="ub2", bufs=1)
+        unread = psum.tile([P, PASS_ROWS // 2], F32, name="ub2", bufs=1)
         for repeat in range(WARM_PASSES):
             nc.tensor.matmul_mx(
                 out=unread[:],
                 lhsT=wg_raw[0][:, 0:P].bitcast(FP8X4),
                 lhsT_scale=w_scales[:].bitcast(U8)[4:P, 0:P],
-                rhs=wg_raw[0][:].bitcast(FP8X4),
-                rhs_scale=w_scales[:].bitcast(U8)[4:P, 0:BANK],
+                rhs=wg_raw[0][:, 0 : PASS_ROWS // 2].bitcast(FP8X4),
+                rhs_scale=w_scales[:].bitcast(U8)[4:P, 0 : PASS_ROWS // 2],
                 start=True,
                 stop=True,
             )
         both = slice(0, PASSES)
-        x_bf = [picked_flat[:, PACK * J - PART : PACK * J + PART].bitcast(BF16)]
-        x_bf.extend(x_stage(part, name) for part, name in ((1, "x_bf1"), (2, "x_bf2")))
-        gather(PACK - 1, 0, PART)
-        gather(PACK - 1, PART, J - PART)
-        for part in range(3):
-            weave_x(part, x_bf[part])
+        x_bf = {0: picked_flat[:, PACK * J - PART : PACK * J].bitcast(BF16)}
+        x_bf[1], x_bf[2] = x_stage(1, "x_bf1"), x_stage(2, "x_bf2")
+        for q in (slice(0, 8), slice(8, 16)):
+            nc.scalar.copy(
+                wg_codes[0][:].bitcast(U32).rearrange("p (t q e) -> p t q e", t=PACK, e=RUN)[:, :, q, :],
+                wg_raw[0][:].bitcast(U32).rearrange("p (q t e) -> p t q e", t=PACK, e=RUN)[:, :, q, :],
+            )
+        gather(PACK - 1, 0, CHUNK)
+        weave_x(0, x_bf[0])
+        gather(PACK - 1, CHUNK, 2 * PART)
+        gather(PACK - 1, 2 * PART, 3 * PART)
+        reorder(wu_codes[0][:], wu_raw[0][:], 2, 1, True)
+        weave_x(1, x_bf[1])
+        weave_x(2, x_bf[2])
         quantize_x(0, x_bf[0])
-        reorder(wg_codes[0][:], wg_raw[0][:], 4, 1)
-        reorder(wu_codes[0][:], wu_raw[0][:], 2, 1)
-        gather(PACK - 1, J - PART, J)
+        wg_codes.append(keep.tile([P, PASS_ROWS], I32, name="wg_codes1", align_bytes=64))
+        wu_codes.append(keep.tile([P, PASS_ROWS // 2], I32, name="wu_codes1", align_bytes=64))
         quantize_x(1, x_bf[1])
-        wg_codes.append(laid.tile([P, PASS_ROWS], I32, name="wg_codes1", offset=relay, align_bytes=64))
-        wu_codes.append(laid.tile([P, PASS_ROWS // 2], I32, name="wu_codes1", offset=relay + 2048, align_bytes=64))
-        x_bf.append(x_stage(3, "x_bf3"))
         reorder(wg_codes[1][:], wg_raw[1][:], 4, 1)
-        weave_x(3, x_bf[3])
         reorder(wu_codes[1][:], wu_raw[1][:], 2, 1)
+        x_bf[3] = x_stage(3, "x_bf3")
+        weave_x(3, x_bf[3])
+        gather(PACK - 1, J - PART, J)
         quantize_x(2, x_bf[2])
         quantize_x(3, x_bf[3])
-        round_wd(0, 4, nc.gpsimd)
-        for step in range(3):
-            gate(step)
-        for step in range(9):
+        x_bf[4] = x_stage(4, "x_bf4")
+        weave_x(4, x_bf[4])
+        gate(0)
+        gate(1)
+        for step in range(10):
             up(step)
+            if step < 9:
+                gate(step + 2)
             multiply(step)
-            if step == 6:
-                round_wd(6, 8, nc.scalar)
-            gate(step + 3)
-        round_wd(4, 6, nc.vector)
-        quantize_wd(0)
+            if step == 1:
+                round_wd(0, 4, nc.gpsimd)
+            if step == 2:
+                round_wd(4, 6, nc.gpsimd)
+        gate(11)
+        round_wd(6, 8, nc.scalar)
+        quantize_x(4, x_bf[4])
         quantize_h(0, both)
-        quantize_wd(2)
+        quantize_wd(0)
         quantize_wd(1)
+        quantize_wd(2)
         quantize_h(1, both)
-        up(9)
-        multiply(9)
+        up(10)
+        up(11)
         gate(12)
         gate(13)
-        up(10)
-        output(0)
-        gate(14)
-        gate(15)
-        multiply(10)
-        up(11)
-        multiply(11)
         up(12)
-        output(1)
+        gate(14)
+        output(0)
+        leave(0, 0)
+        leave(0, 1)
+        up(13)
+        multiply(10)
+        multiply(11)
+        output(1, 0)
+        leave(1, 0)
+        gate(15)
+        up(14)
+        output(1, 1)
+        leave(1, 1)
+        up(15)
         for b in range(PASSES):
             quantize_h(2, slice(b, b + 1))
         weave_y(0, nc.gpsimd)
-        multiply(12)
-        for step in range(13, 16):
-            up(step)
+        for step in range(12, 16):
             multiply(step)
-        weave_y(1, nc.scalar, slice(0, CHUNK))
         output(2)
-        weave_y(1, nc.scalar, slice(CHUNK, PART))
+        leave(2, 0)
+        leave(2, 1)
         quantize_h(3, both)
         quantize_h(4, both)
+        weave_y(1, nc.scalar, slice(0, CHUNK))
         output(3)
+        leave(3, 0)
         output(4)
         planes(0)
+        weave_y(1, nc.vector, slice(CHUNK, PART))
         weave_y(2, nc.vector)
+        leave(4, 0, False)
+        leave(4, 1)
+        weave_y(3, nc.scalar)
         planes(1)
         planes(2)
-        weave_y(3, nc.scalar)
         weave_y(4, nc.vector)
         planes(3)
         planes(4)
@@ -447,6 +485,6 @@ def tile_list_sigm_noneP_kernel(
         for quad in range(4):
             queue = nc.scalar if quad % 2 else nc.sync
             queue.dma_start(
-                out_2[0, 4 * quad : 4 * quad + 4, :].bitcast(I32).rearrange("r (c u) -> c r u", c=4),
-                y_scales[32 * quad : 32 * quad + 16, :].bitcast(I32),
+                out_2[0, 4 * quad : 4 * quad + 4, :].bitcast(I32).rearrange("r (c u) -> c r u", c=2),
+                y_scales[32 * quad : 32 * quad + 8, :].bitcast(I32),
             )

@@ -35,7 +35,7 @@ WD_PARTS = [(0, 4), (4, 6), (6, 8)]
 GATE_BYTES = 4 * BANK
 HELD = (8, 14)
 HELD_BYTES = 3 * GATE_BYTES
-WARM_PASSES = 8
+WARM_PASSES = 4
 
 
 def tile_list_sigm_noneP_kernel(
@@ -379,14 +379,14 @@ def tile_list_sigm_noneP_kernel(
             w_scales[:].bitcast(U32).rearrange("p (b t q e) -> p b t q e", b=PASSES, t=PACK, e=RUN // 4),
             scale_raw[:].bitcast(U32).rearrange("p (b q t e) -> p b t q e", b=PASSES, t=PACK, e=RUN // 4),
         )
-        unread = psum.tile([P, PASS_ROWS // 2], F32, name="ub2", bufs=1)
+        unread = psum.tile([P, BANK], F32, name="ub2", bufs=1)
         for repeat in range(WARM_PASSES):
             nc.tensor.matmul_mx(
                 out=unread[:],
                 lhsT=wg_raw[0][:, 0:P].bitcast(FP8X4),
                 lhsT_scale=w_scales[:].bitcast(U8)[4:P, 0:P],
-                rhs=wg_raw[0][:, 0 : PASS_ROWS // 2].bitcast(FP8X4),
-                rhs_scale=w_scales[:].bitcast(U8)[4:P, 0 : PASS_ROWS // 2],
+                rhs=wg_raw[0][:].bitcast(FP8X4),
+                rhs_scale=w_scales[:].bitcast(U8)[4:P, 0:BANK],
                 start=True,
                 stop=True,
             )

from contextlib import ExitStack

import concourse.mybir as mybir

K, R, N, T, J = 512, 1024, 512, 2048, 1024
FLOPS = 2 * J * (2 * K * R + R * N)

F32 = mybir.dt.float32
BF16 = mybir.dt.bfloat16
I32 = mybir.dt.int32
U32 = mybir.dt.uint32
U16 = mybir.dt.uint16
U8 = mybir.dt.uint8
FP8X4 = mybir.dt.float8_e4m3fn_x4
FP4X4 = mybir.dt.float4_e2m1fn_x4
MULT = mybir.AluOpType.mult
SIGMOID = mybir.ActivationFunctionType.Sigmoid

P = 128
PACK = 4
RUN = 8
PASS_ROWS = P * PACK
PASSES = R // PASS_ROWS
BANK = 512
CHUNK = BANK // PACK
CHUNKS = J // CHUNK
PART = 2 * CHUNK
X_PARTS = [(0, 1), (1, 2), (2, 4), (4, 6), (6, 8)]
GROUPS = [(0, 2), (2, 4), (4, 6), (6, 7), (7, 8)]
STEPS = CHUNKS * PASSES
STEP = [(c, b) for lo, hi in GROUPS for b in range(PASSES) for c in range(lo, hi)]
OUT_TAGS = [("out0", "out1"), ("ga1", "ga2"), ("out1", "out0"), ("ga0",), ("ga1", "ga2")]
WORD_STORES = [(0, 2), (2, 6), (6, 8)]
WD_PARTS = [(0, 4), (4, 6), (6, 8)]
GATE_BYTES = 4 * BANK
HELD = (8, 14)
HELD_BYTES = 3 * GATE_BYTES
WARM_PASSES = 4


def tile_list_sigm_noneP_kernel(
    tc, xT, wgt, wg_words, wg_scales, wu_words, wu_scales, wd, offs, out_0, out_1, out_2
):
    nc = tc.nc
    with ExitStack() as ctx:
        keep = ctx.enter_context(tc.tile_pool(name="keep", bufs=1))
        laid = ctx.enter_context(tc.tile_pool(name="laid", bufs=1))
        psum = ctx.enter_context(tc.psum_pool(name="psum", bufs=1))

        def copy(on_scalar, dst, src):
            if on_scalar:
                nc.scalar.copy(dst, src)
            else:
                nc.vector.tensor_copy(dst, src)

        def quantize(codes, scales, values):
            nc.vector.quantize_mx(out=codes.bitcast(FP8X4), scales=scales, in_=values)

        offsets = keep.tile([P, J // 16], U16, name="offsets")
        scale_raw = keep.tile([P, R // 4], I32, name="scale_raw")
        nc.vector.memset(scale_raw[:], 0)

        def load_scales(source, first_row):
            for quad in range(4):
                rows = slice(32 * quad + first_row, 32 * quad + first_row + 4)
                nc.sync.dma_start(scale_raw[rows, :], source[0, 4 * quad : 4 * quad + 4, :].bitcast(I32))

        x_rows = xT.rearrange("(p i) t -> i p t", i=PACK)
        relay = GATE_BYTES * (STEPS - len(HELD)) + HELD_BYTES * len(HELD)
        x_plane = [keep.tile([P, T], F32, name="x_plane%d" % i) for i in range(PACK)]
        weight = keep.tile([P, J], F32, name="weight", align_bytes=64)
        w_piece = keep.tile([P, J // 16], F32, name="w_piece", align_bytes=64)
        wg_raw = [keep.tile([P, PASS_ROWS], I32, name="wg_raw0", align_bytes=64)]
        wu_raw = [keep.tile([P, PASS_ROWS // 2], I32, name="wu_raw0")]
        wg_raw.append(laid.tile([P, PASS_ROWS], I32, name="wg_raw1", offset=relay, align_bytes=64))
        wu_raw.append(laid.tile([P, PASS_ROWS // 2], I32, name="wu_raw1", offset=relay + 2048, align_bytes=64))
        wd_raw = [keep.tile([P, PACK, N], F32, name="wd_raw%d" % b) for b in range(PASSES)]
        wg_hbm = wg_words[0].rearrange("p r i -> p (r i)").bitcast(I32)
        wu_hbm = wu_words[0].bitcast(I32)

        nc.sync.dma_start(w_piece[:], wgt.rearrange("(g r) (a b) -> g (r a) b", r=16, b=64)[:, ::17, :])
        nc.sync.dma_start(x_plane[0][:], x_rows[0])
        nc.sync.dma_start(offsets[:], offs)
        nc.sync.dma_start(x_plane[1][:], x_rows[1])
        load_scales(wu_scales, 0)
        nc.sync.dma_start(x_plane[2][:], x_rows[2])
        load_scales(wg_scales, 4)
        half = PASS_ROWS // 2
        nc.sync.dma_start(x_plane[3][:], x_rows[3])
        nc.sync.dma_start(wg_raw[0][:, 0:half], wg_hbm[:, 0:half])
        nc.sync.dma_start(wg_raw[0][:, half:PASS_ROWS], wg_hbm[:, half:PASS_ROWS])
        nc.sync.dma_start(wu_raw[0][:], wu_hbm[:, 0:half])

        def load_packed(b):
            nc.sync.dma_start(wg_raw[b][:], wg_hbm[:, PASS_ROWS * b : PASS_ROWS * (b + 1)])
            nc.sync.dma_start(wu_raw[b][:], wu_hbm[:, PASS_ROWS // 2 * b : PASS_ROWS // 2 * (b + 1)])

        def load_wd(b, t):
            rows = wd[PASS_ROWS * b : PASS_ROWS * (b + 1), :].rearrange("(q t e) n -> t q e n", t=PACK, e=RUN)
            nc.sync.dma_start(wd_raw[b][:, t, :], rows[t])

        load_packed(1)
        for s in range(PASSES * PACK):
            load_wd(s // PACK, s % PACK)

        warm = keep.tile([P, 1], F32, name="warm")
        warm_out = keep.tile([P, 1], F32, name="warm_out")
        nc.vector.memset(warm[:], 0.0)
        nc.scalar.activation(warm_out[:], warm[:], SIGMOID)

        turned = keep.tile([P, 2, 32], F32, name="turned", align_bytes=64)
        for s in range(2):
            nc.vector.transpose(turned[:, s, :], w_piece[:, 32 * s : 32 * (s + 1)])
        spread = keep.tile([P, J], F32, name="spread", align_bytes=64)
        for half in range(2):
            cols = slice(J // 2 * half, J // 2 * (half + 1))
            src = turned[:].rearrange("p s (h r) -> p r (s h)", h=2)[:, 8 * half : 8 * (half + 1), :]
            dst = spread[:, cols].rearrange("p (r c e) -> p r c e", r=8, c=4)
            copy(half == 1, dst, src.unsqueeze(3).broadcast_to([P, 8, 4, 16]))
            nc.vector.transpose(weight[:, cols], spread[:, cols])

        picked_flat = keep.tile([P, PACK * J], F32, name="picked", align_bytes=64)
        picked = picked_flat[:].rearrange("p (i j) -> p i j", i=PACK)
        x_codes = keep.tile([P, J], U32, name="x_codes", align_bytes=64)
        def held_at(run):
            return GATE_BYTES * (STEPS - len(HELD)) + HELD_BYTES * run

        def held(run, name, shape, dtype, first):
            return laid.tile(shape, dtype, name=name, offset=held_at(run) + first, align_bytes=64)

        x_scales = {}

        def gather(i, lo, hi):
            window = x_plane[i][:].indirect(offsets[:, lo // 16 : hi // 16])
            nc.vector.tensor_tensor(picked[:, i, lo:hi], window, weight[:, lo:hi], MULT)

        for i in range(PACK - 1):
            gather(i, 0, J)

        def weave(engine, words, planes_of):
            u = 2 if engine is nc.scalar else 4
            src = planes_of.rearrange("p i (s u) -> p s i u", u=u)
            dst = words.rearrange("p (s u i) -> p s i u", u=u, i=PACK)
            if engine is nc.scalar:
                engine.copy(dst, src)
            else:
                engine.tensor_copy(dst, src)

        def weave_x(part, x_bf):
            lo, hi = X_PARTS[part]
            engine = [nc.scalar, nc.scalar, nc.scalar, nc.vector, nc.gpsimd][part]
            weave(engine, x_bf, picked[:, :, CHUNK * lo : CHUNK * hi])

        def quantize_x(part, x_bf):
            lo, hi = X_PARTS[part]
            shape = [P, CHUNK * (hi - lo)]
            if part == 4:
                x_scales[part] = held(0, "x_scales4", shape, U8, 0)
            else:
                x_scales[part] = keep.tile(shape, U8, name="x_scales%d" % part, align_bytes=64)
            quantize(x_codes[:, CHUNK * lo : CHUNK * hi], x_scales[part][:], x_bf)

        def x_stage(part, name):
            lo, hi = X_PARTS[part]
            place = relay + {1: 3072, 2: 4096, 3: 1984, 4: 4096}[part]
            return laid.tile([P, BANK * (hi - lo)], BF16, name=name, offset=place, align_bytes=64)[:]

        w_scales = keep.tile([P, R // 4], I32, name="w_scales", align_bytes=64)
        wg_codes = [keep.tile([P, PASS_ROWS], I32, name="wg_codes0", align_bytes=64)]
        wu_codes = [keep.tile([P, PASS_ROWS // 2], I32, name="wu_codes0", align_bytes=64)]

        def reorder(dst, src, column_bytes, passes, on_scalar=False):
            run = RUN * column_bytes // 4
            dst, src = dst.bitcast(U32), src.bitcast(U32)
            copy(
                on_scalar,
                dst.rearrange("p (b t q e) -> p b t q e", b=passes, t=PACK, e=run),
                src.rearrange("p (b q t e) -> p b t q e", b=passes, t=PACK, e=run),
            )

        wd_codes = keep.tile([P, PASSES, N], U32, name="wd_codes", align_bytes=64)
        wd_scales = {}
        wd_bf = {}

        def wd_part(s):
            return [n for n, (lo, hi) in enumerate(WD_PARTS) if lo <= s < hi][0]

        def round_wd(lo, hi, engine, columns=slice(0, P)):
            part = wd_part(lo)
            first, end = WD_PARTS[part]
            if part not in wd_bf:
                shape = [P, end - first, P, PACK]
                place = GATE_BYTES * (0, 2, 7)[part]
                wd_bf[part] = laid.tile(shape, BF16, name="wd_bf%d" % part, offset=place, align_bytes=64)
            b, i = divmod(lo, PACK)
            src = wd_raw[b][:].rearrange("p t (m i) -> p m t i", i=PACK)[:, columns, :, i : i + hi - lo]
            dst = wd_bf[part][:, lo - first : hi - first, columns, :].rearrange("p i m t -> p m t i")
            if engine is nc.scalar:
                engine.copy(dst, src)
            else:
                engine.tensor_copy(dst, src)

        def quantize_wd(part):
            lo, hi = WD_PARTS[part]
            shape = [P, P * (hi - lo)]
            wd_scales[part] = held(0, "wd_scales%d" % part, shape, U8, (768, 1280, 1536)[part])
            codes = wd_codes[:].rearrange("p b n -> p (b n)")[:, P * lo : P * hi]
            quantize(codes, wd_scales[part][:], wd_bf[part][:].rearrange("p i m t -> p (i m t)"))

        def wd_scale(s):
            first = P * (s - WD_PARTS[wd_part(s)][0])
            return wd_scales[wd_part(s)][:, first : first + P]

        h_codes, h_scales, h_bf = [], {}, []
        for lo, hi in GROUPS:
            width = CHUNK * (hi - lo)
            h_codes.append(keep.tile([P, PASSES, width], U32, name="h_codes%d" % lo, align_bytes=64))
            h_bf.append(keep.tile([P, PASSES, width, PACK], BF16, name="words%d" % lo, align_bytes=64))
        gates = {}

        def bank(tag, slices, width):
            return psum.tile([P, slices, width], F32, name=tag, bufs=1)

        def first_product(step, acc, codes, column_bytes, dtype, scale_row):
            c, b = STEP[step]
            part = [n for n, (lo, hi) in enumerate(X_PARTS) if lo <= c < hi][0]
            inner = slice(CHUNK * (c - X_PARTS[part][0]), CHUNK * (c - X_PARTS[part][0] + 1))
            for t in range(PACK):
                first = b * PASS_ROWS + t * P
                nc.tensor.matmul_mx(
                    out=acc[:, t, :],
                    lhsT=codes[b][:].bitcast(U8)[:, column_bytes * t * P : column_bytes * (t + 1) * P].bitcast(dtype),
                    lhsT_scale=w_scales[:].bitcast(U8)[scale_row:P, first : first + P],
                    rhs=x_codes[:, CHUNK * c : CHUNK * (c + 1)].bitcast(FP8X4),
                    rhs_scale=x_scales[part][:, inner],
                    start=True,
                    stop=True,
                )

        def gate(step):
            ga = bank("out0" if step == STEPS - 1 else "ga%d" % (step % 3), PACK, CHUNK)
            first_product(step, ga, wg_codes, 4, FP8X4, 4)
            if step in HELD:
                place = held_at(HELD.index(step))
            else:
                place = GATE_BYTES * (step - len([other for other in HELD if other < step]))
            gates[step] = laid.tile([P, CHUNK, PACK], F32, name="gate%d" % step, offset=place, align_bytes=64)
            nc.scalar.activation(gates[step][:], ga[:].rearrange("p t j -> p j t"), SIGMOID)

        def group_of(c):
            return [g for g, (lo, hi) in enumerate(GROUPS) if lo <= c < hi][0]

        ups = {}

        def up(step):
            tags = ["ub0", "ub1", "ub2", "out0", "out1"]
            ups[step] = bank(tags[step % 5] if step < 10 else ("ub1", "ub2", "ub0", "ga0", "ub1", "ub2")[step - 10], PACK, CHUNK)
            first_product(step, ups[step], wu_codes, 2, FP4X4, 0)

        def multiply(step):
            c, b = STEP[step]
            g = group_of(c)
            inner = slice(CHUNK * (c - GROUPS[g][0]), CHUNK * (c - GROUPS[g][0] + 1))
            ub = ups[step][:].rearrange("p t j -> p j t")
            nc.vector.tensor_tensor(h_bf[g][:, b, inner, :], ub, gates[step][:], MULT)

        def quantize_h(g, passes):
            width = CHUNK * (GROUPS[g][1] - GROUPS[g][0])
            if g not in h_scales:
                if g == 0:
                    h_scales[g] = held(0, "h_scales0", [P, PASSES, width], U8, 256)
                elif g == 1:
                    h_scales[g] = held(0, "h_scales1", [P, PASSES, width], U8, 1792)
                elif g == 3:
                    h_scales[g] = held(1, "h_scales3", [P, PASSES, width], U8, 0)
                else:
                    h_scales[g] = keep.tile([P, PASSES, width], U8, name="h_scales%d" % g, align_bytes=64)
            quantize(
                h_codes[g][:, passes, :].rearrange("p b j -> p (b j)"),
                h_scales[g][:, passes, :].rearrange("p b j -> p (b j)"),
                h_bf[g][:, passes, :, :].rearrange("p b j t -> p (b j t)"),
            )

        y_scales = keep.tile([P, J // 2], U8, name="y_scales", align_bytes=64)
        y_rows = out_0.rearrange("(p i) j -> p i j", i=PACK)
        word_rows = out_1[0].rearrange("p j i -> p (j i)").bitcast(I32)

        y_tiles, y_banks = {}, {}

        def output(g, only=None):
            lo, hi = GROUPS[g]
            width = CHUNK * (hi - lo)
            last = hi == CHUNKS
            source = group_of(lo)
            inner = slice(CHUNK * (lo - GROUPS[source][0]), CHUNK * (hi - GROUPS[source][0]))
            if g in y_tiles:
                pass
            elif width == PART:
                y_tiles[g] = keep.tile([P, PACK, PART], F32, name="y%d" % lo)[:]
            else:
                if not last:
                    y_tiles["pair"] = keep.tile([P, PACK, PART], F32, name="y%d" % lo)
                y_tiles[g] = y_tiles["pair"][:, :, CHUNK * (lo % 2) : CHUNK * (lo % 2 + 1)]
            per_bank = PACK // 2 if last else BANK // width
            slots = range(PACK // per_bank)
            banks = y_banks.setdefault(g, {})
            slots = slots if only is None else [only]
            for slot in slots:
                banks[slot] = bank(OUT_TAGS[g][slot], per_bank, width)

            def product(i, b, start, stop):
                nc.tensor.matmul_mx(
                    out=banks[i // per_bank][:, i % per_bank, :],
                    lhsT=wd_codes[:, b, P * i : P * (i + 1)].bitcast(FP8X4),
                    lhsT_scale=wd_scale(PACK * b + i),
                    rhs=h_codes[source][:, b, inner].bitcast(FP8X4),
                    rhs_scale=h_scales[source][:, b, inner],
                    start=start,
                    stop=stop,
                )

            if g == 0:
                for b in range(PASSES):
                    for i in range(PACK):
                        product(i, b, b == 0 and i % per_bank == 0, b == PASSES - 1 and i % per_bank == per_bank - 1)
            else:
                for slot in slots:
                    for i in range(slot * per_bank, (slot + 1) * per_bank):
                        for b in range(PASSES):
                            product(i, b, b == 0, b == PASSES - 1)

        def leave(g, slot, on_scalar=True):
            lo, hi = GROUPS[g]
            y, per_bank = y_tiles[g], PACK // len(OUT_TAGS[g])
            part = slice(slot * per_bank, (slot + 1) * per_bank)
            copy(on_scalar, y[:, part, :], y_banks[g][slot][:])
            if hi - lo == 2:
                nc.sync.dma_start(y_rows[:, part, CHUNK * lo : CHUNK * hi], y[:, part, :])
            elif hi == CHUNKS:
                nc.sync.dma_start(y_rows[:, part, J - PART : J], y_tiles["pair"][:, part, :])

        y_bf = {}

        def weave_y(g, engine, picks=None):
            lo, hi = GROUPS[g]
            shape = [P, BANK * (hi - lo)]
            if g in y_bf:
                pass
            elif engine is nc.gpsimd:
                y_bf[g] = keep.tile(shape, BF16, name="words4", align_bytes=64)
            elif g < 3:
                y_bf[g] = keep.tile(shape, BF16, name="words%d" % (5 + g), align_bytes=64)
            else:
                y_bf[g] = keep.tile(shape, BF16, name="y_bf%d" % lo, align_bytes=64)
            if picks:
                weave(engine, y_bf[g][:, PACK * picks.start : PACK * picks.stop], y_tiles[g][:, :, picks])
            else:
                weave(engine, y_bf[g][:], y_tiles[g])

        y_codes, done = {}, []

        def planes(g):
            lo, hi = GROUPS[g]
            first, end = [(a, z) for a, z in WORD_STORES if a <= lo < z][0]
            if first not in y_codes:
                shape = [P, CHUNK * (end - first)]
                if first == 0:
                    y_codes[first] = held(1, "y_codes%d" % first, shape, U32, 256 + 512 * first)
                else:
                    y_codes[first] = keep.tile(shape, U32, name="y_codes%d" % first, align_bytes=64)
            codes = y_codes[first][:, CHUNK * (lo - first) : CHUNK * (hi - first)]
            pair, first_col = divmod(CHUNK * lo, J // 2)
            quantize(codes, y_scales[4 * pair : P, first_col : first_col + CHUNK * (hi - lo)], y_bf[g][:])
            done.append(g)
            if all(n in done for n, (a, e) in enumerate(GROUPS) if first <= a < end):
                nc.sync.dma_start(word_rows[:, CHUNK * first : CHUNK * end], y_codes[first][:].bitcast(I32))

        nc.scalar.copy(
            w_scales[:].bitcast(U32).rearrange("p (b t q e) -> p b t q e", b=PASSES, t=PACK, e=RUN // 4),
            scale_raw[:].bitcast(U32).rearrange("p (b q t e) -> p b t q e", b=PASSES, t=PACK, e=RUN // 4),
        )
        unread = psum.tile([P, BANK], F32, name="ub2", bufs=1)
        for repeat in range(WARM_PASSES):
            nc.tensor.matmul_mx(
                out=unread[:],
                lhsT=wg_raw[0][:, 0:P].bitcast(FP8X4),
                lhsT_scale=w_scales[:].bitcast(U8)[4:P, 0:P],
                rhs=wg_raw[0][:].bitcast(FP8X4),
                rhs_scale=w_scales[:].bitcast(U8)[4:P, 0:BANK],
                start=True,
                stop=True,
            )
        both = slice(0, PASSES)
        x_bf = {0: picked_flat[:, PACK * J - PART : PACK * J].bitcast(BF16)}
        x_bf[1], x_bf[2] = x_stage(1, "x_bf1"), x_stage(2, "x_bf2")
        for q in (slice(0, 8), slice(8, 16)):
            nc.scalar.copy(
                wg_codes[0][:].bitcast(U32).rearrange("p (t q e) -> p t q e", t=PACK, e=RUN)[:, :, q, :],
                wg_raw[0][:].bitcast(U32).rearrange("p (q t e) -> p t q e", t=PACK, e=RUN)[:, :, q, :],
            )
        gather(PACK - 1, 0, CHUNK)
        weave_x(0, x_bf[0])
        gather(PACK - 1, CHUNK, 2 * PART)
        gather(PACK - 1, 2 * PART, 3 * PART)
        reorder(wu_codes[0][:], wu_raw[0][:], 2, 1, True)
        weave_x(1, x_bf[1])
        weave_x(2, x_bf[2])
        quantize_x(0, x_bf[0])
        wg_codes.append(keep.tile([P, PASS_ROWS], I32, name="wg_codes1", align_bytes=64))
        wu_codes.append(keep.tile([P, PASS_ROWS // 2], I32, name="wu_codes1", align_bytes=64))
        quantize_x(1, x_bf[1])
        reorder(wg_codes[1][:], wg_raw[1][:], 4, 1)
        reorder(wu_codes[1][:], wu_raw[1][:], 2, 1)
        x_bf[3] = x_stage(3, "x_bf3")
        weave_x(3, x_bf[3])
        gather(PACK - 1, J - PART, J)
        quantize_x(2, x_bf[2])
        quantize_x(3, x_bf[3])
        x_bf[4] = x_stage(4, "x_bf4")
        weave_x(4, x_bf[4])
        gate(0)
        gate(1)
        for step in range(10):
            up(step)
            if step < 9:
                gate(step + 2)
            multiply(step)
            if step == 1:
                round_wd(0, 4, nc.gpsimd)
            if step == 2:
                round_wd(4, 6, nc.gpsimd)
        gate(11)
        round_wd(6, 8, nc.scalar)
        quantize_x(4, x_bf[4])
        quantize_h(0, both)
        quantize_wd(0)
        quantize_wd(1)
        quantize_wd(2)
        quantize_h(1, both)
        up(10)
        up(11)
        gate(12)
        gate(13)
        up(12)
        gate(14)
        output(0)
        leave(0, 0)
        leave(0, 1)
        up(13)
        multiply(10)
        multiply(11)
        output(1, 0)
        leave(1, 0)
        gate(15)
        up(14)
        output(1, 1)
        leave(1, 1)
        up(15)
        for b in range(PASSES):
            quantize_h(2, slice(b, b + 1))
        weave_y(0, nc.gpsimd)
        for step in range(12, 16):
            multiply(step)
        output(2)
        leave(2, 0)
        leave(2, 1)
        quantize_h(3, both)
        quantize_h(4, both)
        weave_y(1, nc.scalar, slice(0, CHUNK))
        output(3)
        leave(3, 0)
        output(4)
        planes(0)
        weave_y(1, nc.vector, slice(CHUNK, PART))
        weave_y(2, nc.vector)
        leave(4, 0, False)
        leave(4, 1)
        weave_y(3, nc.scalar)
        planes(1)
        planes(2)
        weave_y(4, nc.vector)
        planes(3)
        planes(4)

        for quad in range(4):
            queue = nc.scalar if quad % 2 else nc.sync
            queue.dma_start(
                out_2[0, 4 * quad : 4 * quad + 4, :].bitcast(I32).rearrange("r (c u) -> c r u", c=2),
                y_scales[32 * quad : 32 * quad + 8, :].bitcast(I32),
            )
